import numpy as np
import ml_dtypes


def mxq(x, axis, fmt="e4m3"):
    dtype, down = {"e4m3": (ml_dtypes.float8_e4m3fn, 7), "e5m2": (ml_dtypes.float8_e5m2, 14)}[fmt]
    v = np.moveaxis(np.asarray(x, np.float32).astype(ml_dtypes.bfloat16).astype(np.float64), axis, -1)
    blocks = v.reshape(v.shape[:-1] + (-1, 32))
    amax = np.abs(blocks).max(-1, keepdims=True)
    byte = np.maximum(np.where(amax > 0, np.frexp(amax)[1] - 1 + 127, 0) - down, 1)
    scale = np.exp2(byte - 127.0)
    codes = (blocks / scale).astype(np.float32).astype(dtype).astype(np.float64)
    return np.moveaxis((codes * scale).reshape(v.shape), -1, axis)


WIDE = False


def mx_kscale(k):
    if not WIDE:
        return np.ones(k)
    levels = np.array([10, -10, 5, -5, 0])
    if k % 512:
        return np.exp2(np.random.permutation(np.resize(levels, k // 32))).repeat(32)
    a = np.empty((k // 512, 16))
    for p in range(k // 512):
        a[p, :8] = np.random.permutation(np.resize(levels, 8))
        for g in range(8):
            far = levels[np.abs(levels - a[p, g]) >= 10]
            a[p, g + 8] = far[np.random.randint(len(far))]
    return np.exp2(a.ravel()).repeat(32)


def f64(x):
    return np.asarray(x).astype(np.float64)


def striped(idx):
    return np.tile(idx.reshape(-1, 16).T, (8, 1)).astype(np.uint16)


def unstriped(offs):
    return offs[:16].T.reshape(-1).astype(np.int64)


def silu(v):
    return v / (1.0 + np.exp(-np.maximum(v, -700.0)))


K, T, D, S, V, H, N = 512, 2048, 3, 512, 256, 512, 512
P = 2 ** 7


def setup_inputs():
    n = np.random.standard_normal
    s = mx_kscale(K)[:, None]
    u = mx_kscale(H)
    q = np.random.permutation(S)
    return {
        "xT": (n((K, T)) * s).astype(np.float32),
        "w1": (n((K, H)) / np.sqrt(K) / s * u).astype(np.float32),
        "w2": (n((H, N)) / np.sqrt(H) / u[:, None]).astype(np.float32),
        "gate": np.tile(np.random.uniform(0.2, 1.0, (D, 1, V)) / np.sqrt(D), (1, P, 1)).astype(np.float32),
        "offs": striped(np.random.permutation(T)[:S]),
        "pos1": striped(q[:V]),
        "pos2": striped(q[V:]),
        "pos3": striped(np.random.permutation(S)[:V]),
    }


def reference(xT, w1, w2, gate, offs, pos1, pos2, pos3):
    h = silu(mxq(f64(w1), 0, "e4m3").T @ mxq(f64(xT)[:, unstriped(offs)], 0, "e4m3"))
    z = sum(f64(gate)[d, :1] * h[:, unstriped(p)] for d, p in enumerate((pos1, pos2, pos3)))
    return mxq(f64(w2), 0, "e4m3").T @ mxq(z, 0, "e4m3")

@@ -1,0 +1,179 @@
+from contextlib import ExitStack
+
+import concourse.mybir as mybir
+from concourse.masks import make_identity
+
+FLOPS = 2 * 512 * 512 * 512 + 2 * 512 * 512 * 256
+
+F32 = mybir.dt.float32
+BF16 = mybir.dt.bfloat16
+U32 = mybir.dt.uint32
+U16 = mybir.dt.uint16
+U8 = mybir.dt.uint8
+FP8X4 = mybir.dt.float8_e4m3fn_x4
+MULT = mybir.AluOpType.mult
+ADD = mybir.AluOpType.add
+SILU = mybir.ActivationFunctionType.Silu
+
+P = 128
+K, T, S, V, H, N, D = 512, 2048, 512, 256, 512, 512, 3
+PACK = 4
+
+
+def tile_picked_sage_silu_e_kernel(tc, xT, w1, w2, gate, offs, pos1, pos2, pos3, out):
+    nc = tc.nc
+    with ExitStack() as ctx:
+        keep = ctx.enter_context(tc.tile_pool(name="keep", bufs=1))
+        psum = ctx.enter_context(tc.psum_pool(name="psum", bufs=1))
+
+        offs_t = keep.tile([P, S // 16], U16, name="offs_t")
+        nc.sync.dma_start(offs_t[:], offs)
+        planes = [keep.tile([P, T], F32, name=f"plane{j}") for j in range(PACK)]
+        x_view = xT.rearrange("(p j) t -> p j t", j=PACK)
+        w1_raw = keep.tile([P, PACK, H], F32, name="w1_raw")
+        w2_raw = keep.tile([P, PACK, N], F32, name="w2_raw")
+        gates = keep.tile([P, D, V], F32, name="gates")
+        pos_t = [keep.tile([P, V // 16], U16, name=f"pos_t{d}") for d in range(D)]
+
+        for j in range(PACK):
+            nc.sync.dma_start(planes[j][:], x_view[:, j, :])
+        nc.sync.dma_start(w1_raw[:], w1.rearrange("(p j) c -> p j c", j=PACK))
+        for d, pos in enumerate((pos1, pos2, pos3)):
+            nc.sync.dma_start(gates[:, d, :], gate[d])
+            nc.sync.dma_start(pos_t[d][:], pos)
+        w2_view = w2.rearrange("(g j r) m -> j g r m", j=PACK, r=8)
+        for j in range(PACK):
+            nc.sync.dma_start(w2_raw[:, j, :], w2_view[j])
+
+        warm = keep.tile([P, 1], F32, name="warm")
+        warm_out = keep.tile([P, 1], F32, name="warm_out")
+        nc.vector.memset(warm[:], 0.0)
+        nc.scalar.activation(warm_out[:], warm[:], SILU)
+        ident = keep.tile([P, P], F32, name="ident")
+        make_identity(nc, ident[:])
+
+        xg = keep.tile([P, S, PACK], BF16, align_bytes=64, name="xg")
+        x_codes = keep.tile([P, S], U32, align_bytes=64, name="x_codes")
+        x_scales = keep.tile([P, S], U8, align_bytes=64, name="x_scales")
+        w1g = [keep.tile([P, P, PACK], BF16, align_bytes=64, name=f"w1g{t}") for t in range(4)]
+        w1_codes = [keep.tile([P, P], U32, align_bytes=64, name=f"w1_codes{t}") for t in range(4)]
+        w1_scales = [keep.tile([P, P], U8, align_bytes=64, name=f"w1_scales{t}") for t in range(4)]
+        w2g = keep.tile([P, N, PACK], BF16, align_bytes=64, name="w2g")
+        w2_codes = keep.tile([P, N], U32, align_bytes=64, name="w2_codes")
+        w2_scales = keep.tile([P, N], U8, align_bytes=64, name="w2_scales")
+
+        def quantize(codes, scales, grouped, a, b):
+            nc.vector.quantize_mx(out=codes[:, a:b].bitcast(FP8X4), scales=scales[:, a:b], in_=grouped[:, PACK * a : PACK * b])
+
+        xg_flat = xg[:].rearrange("p s j -> p (s j)")
+        w2g_flat = w2g[:].rearrange("p m j -> p (m j)")
+
+        for j in range(3):
+            nc.vector.tensor_copy(xg[:, :, j], planes[j][:].indirect(offs_t[:]))
+        for u in range(2):
+            nc.vector.tensor_copy(xg[:, 256 * u : 256 * u + 256, 3], planes[3][:].indirect(offs_t[:, 16 * u : 16 * u + 16]))
+        for u in range(2):
+            quantize(x_codes, x_scales, xg_flat, 256 * u, 256 * u + 256)
+
+        w1_in = w1_raw[:].rearrange("p j (g t r) -> t p g r j", t=4, r=8)
+        banks = [psum.tile([P, S], F32, name=f"bank{t}") for t in range(4)]
+        h = [keep.tile([P, S], F32, name=f"h{t}") for t in range(4)]
+
+        def cast_w1(t, copy):
+            grouped = w1g[t][:].rearrange("p (g r) j -> p g r j", r=8)
+            copy(grouped, w1_in[t])
+
+        def quantize_w1(t):
+            quantize(w1_codes[t], w1_scales[t], w1g[t][:].rearrange("p m j -> p (m j)"), 0, P)
+
+        def layer1(bank, t, cols):
+            nc.tensor.matmul_mx(
+                out=bank,
+                lhsT=w1_codes[t][:].bitcast(FP8X4),
+                lhsT_scale=w1_scales[t][:],
+                rhs=x_codes[:, cols].bitcast(FP8X4),
+                rhs_scale=x_scales[:, cols],
+                start=True,
+                stop=True,
+            )
+
+        cast_w1(0, nc.vector.tensor_copy)
+        cast_w1(1, nc.scalar.copy)
+        quantize_w1(0)
+        cast_w1(2, nc.vector.tensor_copy)
+        quantize_w1(1)
+        cast_w1(3, nc.vector.tensor_copy)
+        quantize_w1(2)
+        quantize_w1(3)
+        bank0b = psum.tile([P, 256], F32, name="part0")
+        for u, bank in enumerate((banks[0][:, 0:256], bank0b[:])):
+            cols = slice(256 * u, 256 * u + 256)
+            layer1(bank, 0, cols)
+            nc.scalar.activation(h[0][:, cols], bank, SILU)
+        for t in range(1, 4):
+            layer1(banks[t][:], t, slice(0, S))
+            nc.scalar.activation(h[t][:], banks[t][:], SILU)
+
+        terms = [keep.tile([P, 4, V], F32, name=f"term{d}") for d in range(D)]
+        parts = [psum.tile([P, 4, 128], F32, name=f"part{u}") for u in range(2)]
+
+        def fetch(t, d):
+            nc.vector.tensor_tensor(terms[d][:, t, :], h[t][:].indirect(pos_t[d][:]), gates[:, d, :], MULT)
+
+        def add_two(t):
+            flipped = psum.tile([P, 2, 128], F32, name=f"flipped{t % 2}")
+            for u in range(2):
+                for d in range(2):
+                    nc.tensor.matmul(flipped[:, u, :], terms[d][:, t, 128 * u : 128 * u + 128], ident[:], is_transpose=True, start=d == 0, stop=d == 1)
+            flat = keep.tile([P, 2, 128], F32, name=f"flat{t}")
+            nc.scalar.copy(flat[:], flipped[:])
+            for u in range(2):
+                nc.tensor.transpose(parts[u][:, t, :], flat[:, u, :], ident[:])
+
+        w2_in4 = w2_raw[:].rearrange("p j (c i) -> p c j i", i=4)
+        w2_out4 = w2g[:].rearrange("p (c i) j -> p c j i", i=4)
+
+        for t in range(4):
+            fetch(t, 0)
+            fetch(t, 1)
+            add_two(t)
+            nc.scalar.copy(w2_out4[:, 32 * t : 32 * t + 32], w2_in4[:, 32 * t : 32 * t + 32])
+        for t in range(4):
+            fetch(t, 2)
+            if t < 2:
+                quantize(w2_codes, w2_scales, w2g_flat, 256 * t, 256 * t + 256)
+
+        zg = [keep.tile([P, 128, PACK], BF16, align_bytes=64, name=f"zg{u}") for u in range(2)]
+        z_codes = [keep.tile([P, 128], U32, align_bytes=64, name=f"z_codes{u}") for u in range(2)]
+        z_scales = [keep.tile([P, 128], U8, align_bytes=64, name=f"z_scales{u}") for u in range(2)]
+        for u in range(2):
+            z_out = zg[u][:].rearrange("p (c i) t -> p c t i", i=4)
+            z_in = parts[u][:].rearrange("p t (c i) -> p c t i", i=4)
+            last_in = terms[2][:, :, 128 * u : 128 * u + 128].rearrange("p t (c i) -> p c t i", i=4)
+            nc.vector.tensor_tensor(z_out, z_in, last_in, ADD)
+        for u in range(2):
+            quantize(z_codes[u], z_scales[u], zg[u][:].rearrange("p v j -> p (v j)"), 0, 128)
+
+        staged = [keep.tile([P, 2, 128], F32, name=f"staged{b}") for b in range(4)]
+        out_view = out.rearrange("(m p) v -> p m v", p=P)
+        for u in range(2):
+            for g in range(2):
+                b = 2 * u + g
+                o_bank = psum.tile([P, 2, 128], F32, name=f"bank{b}")
+                for i in range(2):
+                    m = 2 * g + i
+                    nc.tensor.matmul_mx(
+                        out=o_bank[:, i, :],
+                        lhsT=w2_codes[:, 128 * m : 128 * m + 128].bitcast(FP8X4),
+                        lhsT_scale=w2_scales[:, 128 * m : 128 * m + 128],
+                        rhs=z_codes[u][:].bitcast(FP8X4),
+                        rhs_scale=z_scales[u][:],
+                        start=True,
+                        stop=True,
+                    )
+                if b == 2:
+                    nc.vector.tensor_copy(staged[b][:], o_bank[:])
+                else:
+                    nc.scalar.copy(staged[b][:], o_bank[:])
+                queue = nc.scalar if b == 3 else nc.sync
+                queue.dma_start(out_view[:, 2 * g : 2 * g + 2, 128 * u : 128 * u + 128], staged[b][:])

@@ -38,8 +38,8 @@ def tile_picked_sage_silu_e_kernel(tc, xT, w1, w2, gate, offs, pos1, pos2, pos3,
         for j in range(PACK):
             nc.sync.dma_start(planes[j][:], x_view[:, j, :])
         nc.sync.dma_start(w1_raw[:], w1.rearrange("(p j) c -> p j c", j=PACK))
+        nc.sync.dma_start(gates[:], gate.rearrange("d p v -> p d v"))
         for d, pos in enumerate((pos1, pos2, pos3)):
-            nc.sync.dma_start(gates[:, d, :], gate[d])
             nc.sync.dma_start(pos_t[d][:], pos)
         w2_view = w2.rearrange("(g j r) m -> j g r m", j=PACK, r=8)
         for j in range(PACK):
@@ -59,7 +59,6 @@ def tile_picked_sage_silu_e_kernel(tc, xT, w1, w2, gate, offs, pos1, pos2, pos3,
         w1_codes = [keep.tile([P, P], U32, align_bytes=64, name=f"w1_codes{t}") for t in range(4)]
         w1_scales = [keep.tile([P, P], U8, align_bytes=64, name=f"w1_scales{t}") for t in range(4)]
         w2g = keep.tile([P, N, PACK], BF16, align_bytes=64, name="w2g")
-        w2_codes = keep.tile([P, N], U32, align_bytes=64, name="w2_codes")
         w2_scales = keep.tile([P, N], U8, align_bytes=64, name="w2_scales")
 
         def quantize(codes, scales, grouped, a, b):
@@ -125,8 +124,11 @@ def tile_picked_sage_silu_e_kernel(tc, xT, w1, w2, gate, offs, pos1, pos2, pos3,
             for u in range(2):
                 for d in range(2):
                     nc.tensor.matmul(flipped[:, u, :], terms[d][:, t, 128 * u : 128 * u + 128], ident[:], is_transpose=True, start=d == 0, stop=d == 1)
-            flat = keep.tile([P, 2, 128], F32, name=f"flat{t}")
-            nc.scalar.copy(flat[:], flipped[:])
+            if t in (1, 2):
+                flat = w2_raw[:, 0, 256 * (t - 1) : 256 * t].rearrange("p (u v) -> p u v", u=2)
+            else:
+                flat = keep.tile([P, 2, 128], F32, align_bytes=64, name=f"flat{t}")[:]
+            nc.scalar.copy(flat, flipped[:])
             for u in range(2):
                 nc.tensor.transpose(parts[u][:, t, :], flat[:, u, :], ident[:])
 
@@ -136,22 +138,33 @@ def tile_picked_sage_silu_e_kernel(tc, xT, w1, w2, gate, offs, pos1, pos2, pos3,
         for t in range(4):
             fetch(t, 0)
             fetch(t, 1)
+            if t in (1, 2):
+                for m in (2 * t - 2, 2 * t - 1):
+                    nc.scalar.copy(w2_out4[:, 32 * m : 32 * m + 32], w2_in4[:, 32 * m : 32 * m + 32])
             add_two(t)
-            nc.scalar.copy(w2_out4[:, 32 * t : 32 * t + 32], w2_in4[:, 32 * t : 32 * t + 32])
         for t in range(4):
             fetch(t, 2)
-            if t < 2:
-                quantize(w2_codes, w2_scales, w2g_flat, 256 * t, 256 * t + 256)
+        w2_codes = [keep.tile([P, 256], U32, align_bytes=64, name=tag) for tag in ("w2_codes", "flat3")]
+
+        def quantize_w2(a):
+            nc.vector.quantize_mx(
+                out=w2_codes[a][:].bitcast(FP8X4),
+                scales=w2_scales[:, 256 * a : 256 * a + 256],
+                in_=w2g_flat[:, 1024 * a : 1024 * a + 1024],
+            )
 
         zg = [keep.tile([P, 128, PACK], BF16, align_bytes=64, name=f"zg{u}") for u in range(2)]
         z_codes = [keep.tile([P, 128], U32, align_bytes=64, name=f"z_codes{u}") for u in range(2)]
         z_scales = [keep.tile([P, 128], U8, align_bytes=64, name=f"z_scales{u}") for u in range(2)]
         for u in range(2):
+            if u == 0:
+                quantize_w2(0)
             z_out = zg[u][:].rearrange("p (c i) t -> p c t i", i=4)
             z_in = parts[u][:].rearrange("p t (c i) -> p c t i", i=4)
             last_in = terms[2][:, :, 128 * u : 128 * u + 128].rearrange("p t (c i) -> p c t i", i=4)
             nc.vector.tensor_tensor(z_out, z_in, last_in, ADD)
-        for u in range(2):
+            if u == 0:
+                quantize_w2(1)
             quantize(z_codes[u], z_scales[u], zg[u][:].rearrange("p v j -> p (v j)"), 0, 128)
 
         staged = [keep.tile([P, 2, 128], F32, name=f"staged{b}") for b in range(4)]
@@ -164,7 +177,7 @@ def tile_picked_sage_silu_e_kernel(tc, xT, w1, w2, gate, offs, pos1, pos2, pos3,
                     m = 2 * g + i
                     nc.tensor.matmul_mx(
                         out=o_bank[:, i, :],
-                        lhsT=w2_codes[:, 128 * m : 128 * m + 128].bitcast(FP8X4),
+                        lhsT=w2_codes[g][:, 128 * i : 128 * i + 128].bitcast(FP8X4),
                         lhsT_scale=w2_scales[:, 128 * m : 128 * m + 128],
                         rhs=z_codes[u][:].bitcast(FP8X4),
                         rhs_scale=z_scales[u][:],

@@ -74,12 +74,12 @@ def tile_picked_sage_silu_e_kernel(tc, xT, w1, w2, gate, offs, pos1, pos2, pos3,
         for u in range(2):
             quantize(x_codes, x_scales, xg_flat, 256 * u, 256 * u + 256)
 
-        w1_in = w1_raw[:].rearrange("p j (g t r) -> t p g r j", t=4, r=8)
+        w1_in = w1_raw[:].rearrange("p j (g t c i) -> t p g c j i", t=4, c=4, i=2)
         banks = [psum.tile([P, S], F32, name=f"bank{t}") for t in range(4)]
         h = [keep.tile([P, S], F32, name=f"h{t}") for t in range(4)]
 
         def cast_w1(t, copy):
-            grouped = w1g[t][:].rearrange("p (g r) j -> p g r j", r=8)
+            grouped = w1g[t][:].rearrange("p (g c i) j -> p g c j i", c=4, i=2)
             copy(grouped, w1_in[t])
 
         def quantize_w1(t):
@@ -132,15 +132,15 @@ def tile_picked_sage_silu_e_kernel(tc, xT, w1, w2, gate, offs, pos1, pos2, pos3,
             for u in range(2):
                 nc.tensor.transpose(parts[u][:, t, :], flat[:, u, :], ident[:])
 
-        w2_in4 = w2_raw[:].rearrange("p j (c i) -> p c j i", i=4)
-        w2_out4 = w2g[:].rearrange("p (c i) j -> p c j i", i=4)
+        w2_in4 = w2_raw[:].rearrange("p j (c i) -> p c j i", i=2)
+        w2_out4 = w2g[:].rearrange("p (c i) j -> p c j i", i=2)
 
         for t in range(4):
             fetch(t, 0)
             fetch(t, 1)
             if t in (1, 2):
                 for m in (2 * t - 2, 2 * t - 1):
-                    nc.scalar.copy(w2_out4[:, 32 * m : 32 * m + 32], w2_in4[:, 32 * m : 32 * m + 32])
+                    nc.scalar.copy(w2_out4[:, 64 * m : 64 * m + 64], w2_in4[:, 64 * m : 64 * m + 64])
             add_two(t)
         for t in range(4):
             fetch(t, 2)
@@ -159,9 +159,9 @@ def tile_picked_sage_silu_e_kernel(tc, xT, w1, w2, gate, offs, pos1, pos2, pos3,
         for u in range(2):
             if u == 0:
                 quantize_w2(0)
-            z_out = zg[u][:].rearrange("p (c i) t -> p c t i", i=4)
-            z_in = parts[u][:].rearrange("p t (c i) -> p c t i", i=4)
-            last_in = terms[2][:, :, 128 * u : 128 * u + 128].rearrange("p t (c i) -> p c t i", i=4)
+            z_out = zg[u][:].rearrange("p (c i) t -> p c t i", i=2)
+            z_in = parts[u][:].rearrange("p t (c i) -> p c t i", i=2)
+            last_in = terms[2][:, :, 128 * u : 128 * u + 128].rearrange("p t (c i) -> p c t i", i=2)
             nc.vector.tensor_tensor(z_out, z_in, last_in, ADD)
             if u == 0:
                 quantize_w2(1)

@@ -27,7 +27,6 @@ def tile_picked_sage_silu_e_kernel(tc, xT, w1, w2, gate, offs, pos1, pos2, pos3,
         psum = ctx.enter_context(tc.psum_pool(name="psum", bufs=1))
 
         offs_t = keep.tile([P, S // 16], U16, name="offs_t")
-        nc.sync.dma_start(offs_t[:], offs)
         planes = [keep.tile([P, T], F32, name=f"plane{j}") for j in range(PACK)]
         x_view = xT.rearrange("(p j) t -> p j t", j=PACK)
         w1_raw = keep.tile([P, PACK, H], F32, name="w1_raw")
@@ -37,6 +36,8 @@ def tile_picked_sage_silu_e_kernel(tc, xT, w1, w2, gate, offs, pos1, pos2, pos3,
 
         for j in range(PACK):
             nc.sync.dma_start(planes[j][:], x_view[:, j, :])
+            if j == 0:
+                nc.sync.dma_start(offs_t[:], offs)
         nc.sync.dma_start(w1_raw[:], w1.rearrange("(p j) c -> p j c", j=PACK))
         nc.sync.dma_start(gates[:], gate.rearrange("d p v -> p d v"))
         for d, pos in enumerate((pos1, pos2, pos3)):
@@ -75,7 +76,7 @@ def tile_picked_sage_silu_e_kernel(tc, xT, w1, w2, gate, offs, pos1, pos2, pos3,
             quantize(x_codes, x_scales, xg_flat, 256 * u, 256 * u + 256)
 
         w1_in = w1_raw[:].rearrange("p j (g t c i) -> t p g c j i", t=4, c=4, i=2)
-        banks = [psum.tile([P, S], F32, name=f"bank{t}") for t in range(4)]
+        banks = {t: psum.tile([P, S], F32, name=f"bank{t}") for t in range(1, 4)}
         h = [keep.tile([P, S], F32, name=f"h{t}") for t in range(4)]
 
         def cast_w1(t, copy):
@@ -104,11 +105,10 @@ def tile_picked_sage_silu_e_kernel(tc, xT, w1, w2, gate, offs, pos1, pos2, pos3,
         cast_w1(3, nc.vector.tensor_copy)
         quantize_w1(2)
         quantize_w1(3)
-        bank0b = psum.tile([P, 256], F32, name="part0")
-        for u, bank in enumerate((banks[0][:, 0:256], bank0b[:])):
-            cols = slice(256 * u, 256 * u + 256)
-            layer1(bank, 0, cols)
-            nc.scalar.activation(h[0][:, cols], bank, SILU)
+        for tag, a, b in (("part0", 0, 128), ("part1", 128, 256), ("bank0", 256, 512)):
+            bank = psum.tile([P, b - a], F32, name=tag)
+            layer1(bank[:], 0, slice(a, b))
+            nc.scalar.activation(h[0][:, a:b], bank[:], SILU)
         for t in range(1, 4):
             layer1(banks[t][:], t, slice(0, S))
             nc.scalar.activation(h[t][:], banks[t][:], SILU)
@@ -167,26 +167,30 @@ def tile_picked_sage_silu_e_kernel(tc, xT, w1, w2, gate, offs, pos1, pos2, pos3,
                 quantize_w2(1)
             quantize(z_codes[u], z_scales[u], zg[u][:].rearrange("p v j -> p (v j)"), 0, 128)
 
-        staged = [keep.tile([P, 2, 128], F32, name=f"staged{b}") for b in range(4)]
+        def layer2(bank, m, u):
+            nc.tensor.matmul_mx(
+                out=bank,
+                lhsT=w2_codes[m // 2][:, 128 * (m % 2) : 128 * (m % 2) + 128].bitcast(FP8X4),
+                lhsT_scale=w2_scales[:, 128 * m : 128 * m + 128],
+                rhs=z_codes[u][:].bitcast(FP8X4),
+                rhs_scale=z_scales[u][:],
+                start=True,
+                stop=True,
+            )
+
         out_view = out.rearrange("(m p) v -> p m v", p=P)
-        for u in range(2):
-            for g in range(2):
-                b = 2 * u + g
-                o_bank = psum.tile([P, 2, 128], F32, name=f"bank{b}")
-                for i in range(2):
-                    m = 2 * g + i
-                    nc.tensor.matmul_mx(
-                        out=o_bank[:, i, :],
-                        lhsT=w2_codes[g][:, 128 * i : 128 * i + 128].bitcast(FP8X4),
-                        lhsT_scale=w2_scales[:, 128 * m : 128 * m + 128],
-                        rhs=z_codes[u][:].bitcast(FP8X4),
-                        rhs_scale=z_scales[u][:],
-                        start=True,
-                        stop=True,
-                    )
-                if b == 2:
-                    nc.vector.tensor_copy(staged[b][:], o_bank[:])
-                else:
-                    nc.scalar.copy(staged[b][:], o_bank[:])
-                queue = nc.scalar if b == 3 else nc.sync
-                queue.dma_start(out_view[:, 2 * g : 2 * g + 2, 128 * u : 128 * u + 128], staged[b][:])
+        for g in range(2):
+            o_bank = psum.tile([P, 2, 128], F32, name=f"flipped{g}")
+            for i in range(2):
+                layer2(o_bank[:, i, :], 2 * g + i, 0)
+            staged = keep.tile([P, 2, 128], F32, name=f"staged{g}")
+            nc.scalar.copy(staged[:], o_bank[:])
+            nc.sync.dma_start(out_view[:, 2 * g : 2 * g + 2, 0:128], staged[:])
+        for m in range(4):
+            o_bank = psum.tile([P, 128], F32, name=f"bank{m}")
+            layer2(o_bank[:], m, 1)
+            staged = keep.tile([P, 128], F32, name=f"staged_last{m}")
+            copy = (nc.vector.tensor_copy, nc.scalar.copy)[m % 2]
+            copy(staged[:], o_bank[:])
+            queue = nc.scalar if m == 3 else nc.sync
+            queue.dma_start(out_view[:, m, 128:256], staged[:])

@@ -18,6 +18,7 @@ SILU = mybir.ActivationFunctionType.Silu
 P = 128
 K, T, S, V, H, N, D = 512, 2048, 512, 256, 512, 512, 3
 PACK = 4
+CASTS = ((0,), (1, 2), (3,), ())
 
 
 def tile_picked_sage_silu_e_kernel(tc, xT, w1, w2, gate, offs, pos1, pos2, pos3, out):
@@ -27,6 +28,7 @@ def tile_picked_sage_silu_e_kernel(tc, xT, w1, w2, gate, offs, pos1, pos2, pos3,
         psum = ctx.enter_context(tc.psum_pool(name="psum", bufs=1))
 
         offs_t = keep.tile([P, S // 16], U16, name="offs_t")
+        nc.sync.dma_start(offs_t[:], offs)
         planes = [keep.tile([P, T], F32, name=f"plane{j}") for j in range(PACK)]
         x_view = xT.rearrange("(p j) t -> p j t", j=PACK)
         w1_raw = keep.tile([P, PACK, H], F32, name="w1_raw")
@@ -36,8 +38,6 @@ def tile_picked_sage_silu_e_kernel(tc, xT, w1, w2, gate, offs, pos1, pos2, pos3,
 
         for j in range(PACK):
             nc.sync.dma_start(planes[j][:], x_view[:, j, :])
-            if j == 0:
-                nc.sync.dma_start(offs_t[:], offs)
         nc.sync.dma_start(w1_raw[:], w1.rearrange("(p j) c -> p j c", j=PACK))
         nc.sync.dma_start(gates[:], gate.rearrange("d p v -> p d v"))
         for d, pos in enumerate((pos1, pos2, pos3)):
@@ -124,13 +124,21 @@ def tile_picked_sage_silu_e_kernel(tc, xT, w1, w2, gate, offs, pos1, pos2, pos3,
             for u in range(2):
                 for d in range(2):
                     nc.tensor.matmul(flipped[:, u, :], terms[d][:, t, 128 * u : 128 * u + 128], ident[:], is_transpose=True, start=d == 0, stop=d == 1)
-            if t in (1, 2):
-                flat = w2_raw[:, 0, 256 * (t - 1) : 256 * t].rearrange("p (u v) -> p u v", u=2)
-            else:
-                flat = keep.tile([P, 2, 128], F32, align_bytes=64, name=f"flat{t}")[:]
+            m = CASTS[t][-1]
+            flat = w2_raw[:, 0:2, 128 * m : 128 * m + 128]
             nc.scalar.copy(flat, flipped[:])
             for u in range(2):
                 nc.tensor.transpose(parts[u][:, t, :], flat[:, u, :], ident[:])
+
+        def add_two_last(t):
+            halves = [psum.tile([P, 128], F32, name=tag) for tag in ("flipped1", "flipped0")]
+            for d in range(2):
+                for u in range(2):
+                    nc.tensor.matmul(halves[u][:], terms[d][:, t, 128 * u : 128 * u + 128], ident[:], is_transpose=True, start=d == 0, stop=d == 1)
+            for u in range(2):
+                flat = keep.tile([P, 128], F32, align_bytes=64, name=f"flat_last{u}")
+                nc.scalar.copy(flat[:], halves[u][:])
+                nc.tensor.transpose(parts[u][:, t, :], flat[:], ident[:])
 
         w2_in4 = w2_raw[:].rearrange("p j (c i) -> p c j i", i=2)
         w2_out4 = w2g[:].rearrange("p (c i) j -> p c j i", i=2)
@@ -138,13 +146,12 @@ def tile_picked_sage_silu_e_kernel(tc, xT, w1, w2, gate, offs, pos1, pos2, pos3,
         for t in range(4):
             fetch(t, 0)
             fetch(t, 1)
-            if t in (1, 2):
-                for m in (2 * t - 2, 2 * t - 1):
-                    nc.scalar.copy(w2_out4[:, 64 * m : 64 * m + 64], w2_in4[:, 64 * m : 64 * m + 64])
-            add_two(t)
+            for m in CASTS[t]:
+                nc.scalar.copy(w2_out4[:, 64 * m : 64 * m + 64], w2_in4[:, 64 * m : 64 * m + 64])
+            (add_two if t < 3 else add_two_last)(t)
         for t in range(4):
             fetch(t, 2)
-        w2_codes = [keep.tile([P, 256], U32, align_bytes=64, name=tag) for tag in ("w2_codes", "flat3")]
+        w2_codes = [keep.tile([P, 256], U32, align_bytes=64, name=tag) for tag in ("w2_codes", "flat_last0")]
 
         def quantize_w2(a):
             nc.vector.quantize_mx(

@@ -28,7 +28,6 @@ def tile_picked_sage_silu_e_kernel(tc, xT, w1, w2, gate, offs, pos1, pos2, pos3,
         psum = ctx.enter_context(tc.psum_pool(name="psum", bufs=1))
 
         offs_t = keep.tile([P, S // 16], U16, name="offs_t")
-        nc.sync.dma_start(offs_t[:], offs)
         planes = [keep.tile([P, T], F32, name=f"plane{j}") for j in range(PACK)]
         x_view = xT.rearrange("(p j) t -> p j t", j=PACK)
         w1_raw = keep.tile([P, PACK, H], F32, name="w1_raw")
@@ -38,13 +37,14 @@ def tile_picked_sage_silu_e_kernel(tc, xT, w1, w2, gate, offs, pos1, pos2, pos3,
 
         for j in range(PACK):
             nc.sync.dma_start(planes[j][:], x_view[:, j, :])
+            if j == 0:
+                nc.sync.dma_start(offs_t[:], offs)
         nc.sync.dma_start(w1_raw[:], w1.rearrange("(p j) c -> p j c", j=PACK))
+        nc.sync.dma_start(pos_t[0][:], pos1)
         nc.sync.dma_start(gates[:], gate.rearrange("d p v -> p d v"))
-        for d, pos in enumerate((pos1, pos2, pos3)):
-            nc.sync.dma_start(pos_t[d][:], pos)
-        w2_view = w2.rearrange("(g j r) m -> j g r m", j=PACK, r=8)
-        for j in range(PACK):
-            nc.sync.dma_start(w2_raw[:, j, :], w2_view[j])
+        nc.sync.dma_start(pos_t[1][:], pos2)
+        nc.sync.dma_start(w2_raw[:], w2.rearrange("(p j) m -> p j m", j=PACK))
+        nc.sync.dma_start(pos_t[2][:], pos3)
 
         warm = keep.tile([P, 1], F32, name="warm")
         warm_out = keep.tile([P, 1], F32, name="warm_out")
@@ -56,7 +56,7 @@ def tile_picked_sage_silu_e_kernel(tc, xT, w1, w2, gate, offs, pos1, pos2, pos3,
         xg = keep.tile([P, S, PACK], BF16, align_bytes=64, name="xg")
         x_codes = keep.tile([P, S], U32, align_bytes=64, name="x_codes")
         x_scales = keep.tile([P, S], U8, align_bytes=64, name="x_scales")
-        w1g = [keep.tile([P, P, PACK], BF16, align_bytes=64, name=f"w1g{t}") for t in range(4)]
+        w1g = [keep.tile([P, 2, P, PACK], BF16, align_bytes=64, name=f"w1g{a}") for a in range(2)]
         w1_codes = [keep.tile([P, P], U32, align_bytes=64, name=f"w1_codes{t}") for t in range(4)]
         w1_scales = [keep.tile([P, P], U8, align_bytes=64, name=f"w1_scales{t}") for t in range(4)]
         w2g = keep.tile([P, N, PACK], BF16, align_bytes=64, name="w2g")
@@ -75,16 +75,15 @@ def tile_picked_sage_silu_e_kernel(tc, xT, w1, w2, gate, offs, pos1, pos2, pos3,
         for u in range(2):
             quantize(x_codes, x_scales, xg_flat, 256 * u, 256 * u + 256)
 
-        w1_in = w1_raw[:].rearrange("p j (g t c i) -> t p g c j i", t=4, c=4, i=2)
+        w1_in = w1_raw[:].rearrange("p j (m a t) -> a p m j t", a=2, t=2)
         banks = {t: psum.tile([P, S], F32, name=f"bank{t}") for t in range(1, 4)}
         h = [keep.tile([P, S], F32, name=f"h{t}") for t in range(4)]
 
-        def cast_w1(t, copy):
-            grouped = w1g[t][:].rearrange("p (g c i) j -> p g c j i", c=4, i=2)
-            copy(grouped, w1_in[t])
+        def cast_w1(a, copy, m0, m1):
+            copy(w1g[a][:].rearrange("p t m j -> p m j t")[:, m0:m1], w1_in[a][:, m0:m1])
 
         def quantize_w1(t):
-            quantize(w1_codes[t], w1_scales[t], w1g[t][:].rearrange("p m j -> p (m j)"), 0, P)
+            quantize(w1_codes[t], w1_scales[t], w1g[t // 2][:, t % 2].rearrange("p m j -> p (m j)"), 0, P)
 
         def layer1(bank, t, cols):
             nc.tensor.matmul_mx(
@@ -97,14 +96,12 @@ def tile_picked_sage_silu_e_kernel(tc, xT, w1, w2, gate, offs, pos1, pos2, pos3,
                 stop=True,
             )
 
-        cast_w1(0, nc.vector.tensor_copy)
-        cast_w1(1, nc.scalar.copy)
-        quantize_w1(0)
-        cast_w1(2, nc.vector.tensor_copy)
-        quantize_w1(1)
-        cast_w1(3, nc.vector.tensor_copy)
-        quantize_w1(2)
-        quantize_w1(3)
+        cast_w1(0, nc.vector.tensor_copy, 0, 80)
+        cast_w1(0, nc.scalar.copy, 80, P)
+        cast_w1(1, nc.vector.tensor_copy, 0, 48)
+        cast_w1(1, nc.scalar.copy, 48, P)
+        for t in range(4):
+            quantize_w1(t)
         for tag, a, b in (("part0", 0, 128), ("part1", 128, 256), ("bank0", 256, 512)):
             bank = psum.tile([P, b - a], F32, name=tag)
             layer1(bank[:], 0, slice(a, b))

@@ -18,7 +18,6 @@ SILU = mybir.ActivationFunctionType.Silu
 P = 128
 K, T, S, V, H, N, D = 512, 2048, 512, 256, 512, 512, 3
 PACK = 4
-CASTS = ((0,), (1, 2), (3,), ())
 
 
 def tile_picked_sage_silu_e_kernel(tc, xT, w1, w2, gate, offs, pos1, pos2, pos3, out):
@@ -30,7 +29,8 @@ def tile_picked_sage_silu_e_kernel(tc, xT, w1, w2, gate, offs, pos1, pos2, pos3,
         offs_t = keep.tile([P, S // 16], U16, name="offs_t")
         planes = [keep.tile([P, T], F32, name=f"plane{j}") for j in range(PACK)]
         x_view = xT.rearrange("(p j) t -> p j t", j=PACK)
-        w1_raw = keep.tile([P, PACK, H], F32, name="w1_raw")
+        w1_view = w1.rearrange("(p j) c -> p j c", j=PACK)
+        w1_raw = [keep.tile([P, PACK, 256], F32, name=f"w1_raw{b}") for b in range(2)]
         w2_raw = keep.tile([P, PACK, N], F32, name="w2_raw")
         gates = keep.tile([P, D, V], F32, name="gates")
         pos_t = [keep.tile([P, V // 16], U16, name=f"pos_t{d}") for d in range(D)]
@@ -39,12 +39,13 @@ def tile_picked_sage_silu_e_kernel(tc, xT, w1, w2, gate, offs, pos1, pos2, pos3,
             nc.sync.dma_start(planes[j][:], x_view[:, j, :])
             if j == 0:
                 nc.sync.dma_start(offs_t[:], offs)
-        nc.sync.dma_start(w1_raw[:], w1.rearrange("(p j) c -> p j c", j=PACK))
-        nc.sync.dma_start(pos_t[0][:], pos1)
-        nc.sync.dma_start(gates[:], gate.rearrange("d p v -> p d v"))
-        nc.sync.dma_start(pos_t[1][:], pos2)
+        for b in range(2):
+            nc.sync.dma_start(w1_raw[b][:], w1_view[:, :, 256 * b : 256 * b + 256])
+        for d, pos in enumerate((pos1, pos2, pos3)):
+            nc.sync.dma_start(pos_t[d][:], pos)
+            if d == 2:
+                nc.sync.dma_start(gates[:], gate.rearrange("d p v -> p d v"))
         nc.sync.dma_start(w2_raw[:], w2.rearrange("(p j) m -> p j m", j=PACK))
-        nc.sync.dma_start(pos_t[2][:], pos3)
 
         warm = keep.tile([P, 1], F32, name="warm")
         warm_out = keep.tile([P, 1], F32, name="warm_out")
@@ -52,13 +53,16 @@ def tile_picked_sage_silu_e_kernel(tc, xT, w1, w2, gate, offs, pos1, pos2, pos3,
         nc.scalar.activation(warm_out[:], warm[:], SILU)
         ident = keep.tile([P, P], F32, name="ident")
         make_identity(nc, ident[:])
+        third = keep.tile([P, 4, V], F32, name="third")
+        nc.vector.memset(third[:, 0:2, :], 0.0)
 
         xg = keep.tile([P, S, PACK], BF16, align_bytes=64, name="xg")
         x_codes = keep.tile([P, S], U32, align_bytes=64, name="x_codes")
         x_scales = keep.tile([P, S], U8, align_bytes=64, name="x_scales")
-        w1g = [keep.tile([P, 2, P, PACK], BF16, align_bytes=64, name=f"w1g{a}") for a in range(2)]
-        w1_codes = [keep.tile([P, P], U32, align_bytes=64, name=f"w1_codes{t}") for t in range(4)]
-        w1_scales = [keep.tile([P, P], U8, align_bytes=64, name=f"w1_scales{t}") for t in range(4)]
+        w1g_low = [keep.tile([P, 2, 64, PACK], BF16, align_bytes=64, name=f"w1g_low{b}") for b in range(2)]
+        w1g_high = keep.tile([P, 2, P, PACK], BF16, align_bytes=64, name="w1g_high")
+        w1_codes = [keep.tile([P, w], U32, align_bytes=64, name=f"w1_codes{t}") for t, w in enumerate((P, P, 2 * P))]
+        w1_scales = [keep.tile([P, w], U8, align_bytes=64, name=f"w1_scales{t}") for t, w in enumerate((P, P, 2 * P))]
         w2g = keep.tile([P, N, PACK], BF16, align_bytes=64, name="w2g")
         w2_scales = keep.tile([P, N], U8, align_bytes=64, name="w2_scales")
 
@@ -72,37 +76,40 @@ def tile_picked_sage_silu_e_kernel(tc, xT, w1, w2, gate, offs, pos1, pos2, pos3,
             nc.vector.tensor_copy(xg[:, :, j], planes[j][:].indirect(offs_t[:]))
         for u in range(2):
             nc.vector.tensor_copy(xg[:, 256 * u : 256 * u + 256, 3], planes[3][:].indirect(offs_t[:, 16 * u : 16 * u + 16]))
-        for u in range(2):
-            quantize(x_codes, x_scales, xg_flat, 256 * u, 256 * u + 256)
 
-        w1_in = w1_raw[:].rearrange("p j (m a t) -> a p m j t", a=2, t=2)
+        w1_in = [w1_raw[b][:].rearrange("p j (m a t) -> a p m j t", a=2, t=2) for b in range(2)]
         banks = {t: psum.tile([P, S], F32, name=f"bank{t}") for t in range(1, 4)}
         h = [keep.tile([P, S], F32, name=f"h{t}") for t in range(4)]
 
-        def cast_w1(a, copy, m0, m1):
-            copy(w1g[a][:].rearrange("p t m j -> p m j t")[:, m0:m1], w1_in[a][:, m0:m1])
+        def cast_low(b, copy):
+            copy(w1g_low[b][:].rearrange("p t m j -> p m j t"), w1_in[b][0])
 
-        def quantize_w1(t):
-            quantize(w1_codes[t], w1_scales[t], w1g[t // 2][:, t % 2].rearrange("p m j -> p (m j)"), 0, P)
+        def cast_high(b, copy):
+            copy(w1g_high[:].rearrange("p t m j -> p m j t")[:, 64 * b : 64 * b + 64], w1_in[b][1])
 
         def layer1(bank, t, cols):
+            w = min(t, 2)
+            c = slice(P * (t - w), P * (t - w) + P)
             nc.tensor.matmul_mx(
                 out=bank,
-                lhsT=w1_codes[t][:].bitcast(FP8X4),
-                lhsT_scale=w1_scales[t][:],
+                lhsT=w1_codes[w][:, c].bitcast(FP8X4),
+                lhsT_scale=w1_scales[w][:, c],
                 rhs=x_codes[:, cols].bitcast(FP8X4),
                 rhs_scale=x_scales[:, cols],
                 start=True,
                 stop=True,
             )
 
-        cast_w1(0, nc.vector.tensor_copy, 0, 80)
-        cast_w1(0, nc.scalar.copy, 80, P)
-        cast_w1(1, nc.vector.tensor_copy, 0, 48)
-        cast_w1(1, nc.scalar.copy, 48, P)
-        for t in range(4):
-            quantize_w1(t)
-        for tag, a, b in (("part0", 0, 128), ("part1", 128, 256), ("bank0", 256, 512)):
+        cast_low(0, nc.scalar.copy)
+        cast_high(0, nc.scalar.copy)
+        quantize(x_codes, x_scales, xg_flat, 0, 256)
+        quantize(w1_codes[0], w1_scales[0], w1g_low[0][:].rearrange("p t m j -> p (t m j)"), 0, P)
+        quantize(x_codes, x_scales, xg_flat, 256, 512)
+        cast_low(1, nc.vector.tensor_copy)
+        cast_high(1, nc.vector.tensor_copy)
+        quantize(w1_codes[1], w1_scales[1], w1g_low[1][:].rearrange("p t m j -> p (t m j)"), 0, P)
+        quantize(w1_codes[2], w1_scales[2], w1g_high[:].rearrange("p t m j -> p (t m j)"), 0, 2 * P)
+        for tag, a, b in (("part0", 0, 256), ("bank0", 256, 512)):
             bank = psum.tile([P, b - a], F32, name=tag)
             layer1(bank[:], 0, slice(a, b))
             nc.scalar.activation(h[0][:, a:b], bank[:], SILU)
@@ -110,44 +117,60 @@ def tile_picked_sage_silu_e_kernel(tc, xT, w1, w2, gate, offs, pos1, pos2, pos3,
             layer1(banks[t][:], t, slice(0, S))
             nc.scalar.activation(h[t][:], banks[t][:], SILU)
 
-        terms = [keep.tile([P, 4, V], F32, name=f"term{d}") for d in range(D)]
+        terms = [keep.tile([P, 4 if d < 2 else 2, V], F32, name=f"term{d}") for d in range(D)]
         parts = [psum.tile([P, 4, 128], F32, name=f"part{u}") for u in range(2)]
 
-        def fetch(t, d):
-            nc.vector.tensor_tensor(terms[d][:, t, :], h[t][:].indirect(pos_t[d][:]), gates[:, d, :], MULT)
+        def fetch(dest, t, d):
+            nc.vector.tensor_tensor(dest, h[t][:].indirect(pos_t[d][:]), gates[:, d, :], MULT)
 
-        def add_two(t):
-            flipped = psum.tile([P, 2, 128], F32, name=f"flipped{t % 2}")
-            for u in range(2):
-                for d in range(2):
-                    nc.tensor.matmul(flipped[:, u, :], terms[d][:, t, 128 * u : 128 * u + 128], ident[:], is_transpose=True, start=d == 0, stop=d == 1)
-            m = CASTS[t][-1]
-            flat = w2_raw[:, 0:2, 128 * m : 128 * m + 128]
-            nc.scalar.copy(flat, flipped[:])
-            for u in range(2):
-                nc.tensor.transpose(parts[u][:, t, :], flat[:, u, :], ident[:])
-
-        def add_two_last(t):
-            halves = [psum.tile([P, 128], F32, name=tag) for tag in ("flipped1", "flipped0")]
-            for d in range(2):
-                for u in range(2):
-                    nc.tensor.matmul(halves[u][:], terms[d][:, t, 128 * u : 128 * u + 128], ident[:], is_transpose=True, start=d == 0, stop=d == 1)
-            for u in range(2):
-                flat = keep.tile([P, 128], F32, align_bytes=64, name=f"flat_last{u}")
-                nc.scalar.copy(flat[:], halves[u][:])
-                nc.tensor.transpose(parts[u][:, t, :], flat[:], ident[:])
+        def flip(bank, t, d, u, last):
+            nc.tensor.matmul(bank, terms[d][:, t, 128 * u : 128 * u + 128], ident[:], is_transpose=True, start=d == 0, stop=d == last)
 
         w2_in4 = w2_raw[:].rearrange("p j (c i) -> p c j i", i=2)
         w2_out4 = w2g[:].rearrange("p (c i) j -> p c j i", i=2)
 
-        for t in range(4):
-            fetch(t, 0)
-            fetch(t, 1)
-            for m in CASTS[t]:
-                nc.scalar.copy(w2_out4[:, 64 * m : 64 * m + 64], w2_in4[:, 64 * m : 64 * m + 64])
-            (add_two if t < 3 else add_two_last)(t)
-        for t in range(4):
-            fetch(t, 2)
+        def cast_w2(m):
+            nc.scalar.copy(w2_out4[:, 64 * m : 64 * m + 64], w2_in4[:, 64 * m : 64 * m + 64])
+
+        flat_low = w2_raw[:, :, 64:192]
+        for t in range(2):
+            for d in range(D):
+                fetch(terms[d][:, t, :], t, d)
+            cast_w2(t)
+            flipped = psum.tile([P, 2, 128], F32, name=f"flipped{t}")
+            for u in range(2):
+                for d in range(D):
+                    flip(flipped[:, u, :], t, d, u, 2)
+            nc.scalar.copy(flat_low[:, :, 64 * t : 64 * t + 64], flipped[:].rearrange("p u (s m) -> p (u s) m", s=2))
+        for u in range(2):
+            for s in range(2):
+                nc.tensor.transpose(parts[u][:, s, :], flat_low[:, 2 * u + s, :], ident[:])
+
+        for d in range(2):
+            fetch(terms[d][:, 2, :], 2, d)
+        cast_w2(2)
+        cast_w2(3)
+        flipped = psum.tile([P, 2, 128], F32, name="flipped0")
+        for u in range(2):
+            for d in range(2):
+                flip(flipped[:, u, :], 2, d, u, 1)
+        flat = w2_raw[:, 0:2, 384:512]
+        nc.scalar.copy(flat, flipped[:])
+        for u in range(2):
+            nc.tensor.transpose(parts[u][:, 2, :], flat[:, u, :], ident[:])
+
+        for d in range(2):
+            fetch(terms[d][:, 3, :], 3, d)
+        halves = [psum.tile([P, 128], F32, name=tag) for tag in ("flipped1", "flipped0")]
+        for d in range(2):
+            for u in range(2):
+                flip(halves[u][:], 3, d, u, 1)
+        for u in range(2):
+            flat = keep.tile([P, 128], F32, align_bytes=64, name=f"flat_last{u}")
+            nc.scalar.copy(flat[:], halves[u][:])
+            nc.tensor.transpose(parts[u][:, 3, :], flat[:], ident[:])
+        for t in range(2, 4):
+            fetch(third[:, t, :], t, 2)
         w2_codes = [keep.tile([P, 256], U32, align_bytes=64, name=tag) for tag in ("w2_codes", "flat_last0")]
 
         def quantize_w2(a):
@@ -165,7 +188,7 @@ def tile_picked_sage_silu_e_kernel(tc, xT, w1, w2, gate, offs, pos1, pos2, pos3,
                 quantize_w2(0)
             z_out = zg[u][:].rearrange("p (c i) t -> p c t i", i=2)
             z_in = parts[u][:].rearrange("p t (c i) -> p c t i", i=2)
-            last_in = terms[2][:, :, 128 * u : 128 * u + 128].rearrange("p t (c i) -> p c t i", i=2)
+            last_in = third[:, :, 128 * u : 128 * u + 128].rearrange("p t (c i) -> p c t i", i=2)
             nc.vector.tensor_tensor(z_out, z_in, last_in, ADD)
             if u == 0:
                 quantize_w2(1)

@@ -35,16 +35,17 @@ def tile_picked_sage_silu_e_kernel(tc, xT, w1, w2, gate, offs, pos1, pos2, pos3,
         gates = keep.tile([P, D, V], F32, name="gates")
         pos_t = [keep.tile([P, V // 16], U16, name=f"pos_t{d}") for d in range(D)]
 
+        gate_rows = keep.tile([P, V], F32, name="gate_rows")
+        nc.gpsimd.memset(gate_rows[:], 0.0)
         for j in range(PACK):
             nc.sync.dma_start(planes[j][:], x_view[:, j, :])
             if j == 0:
+                nc.sync.dma_start(gate_rows[0:D, :], gate[:, 0, :])
                 nc.sync.dma_start(offs_t[:], offs)
         for b in range(2):
             nc.sync.dma_start(w1_raw[b][:], w1_view[:, :, 256 * b : 256 * b + 256])
         for d, pos in enumerate((pos1, pos2, pos3)):
             nc.sync.dma_start(pos_t[d][:], pos)
-            if d == 2:
-                nc.sync.dma_start(gates[:], gate.rearrange("d p v -> p d v"))
         nc.sync.dma_start(w2_raw[:], w2.rearrange("(p j) m -> p j m", j=PACK))
 
         warm = keep.tile([P, 1], F32, name="warm")
@@ -53,6 +54,16 @@ def tile_picked_sage_silu_e_kernel(tc, xT, w1, w2, gate, offs, pos1, pos2, pos3,
         nc.scalar.activation(warm_out[:], warm[:], SILU)
         ident = keep.tile([P, P], F32, name="ident")
         make_identity(nc, ident[:])
+        turned = psum.tile([P, 2, P], F32, name="bank1")
+        for u in range(2):
+            nc.tensor.transpose(turned[:, u, :], gate_rows[:, P * u : P * u + P], ident[:])
+        gate_cols = keep.tile([P, 2, D], F32, name="gate_cols")
+        nc.scalar.copy(gate_cols[:], turned[:, :, 0:D])
+        for d in range(D):
+            spread = psum.tile([P, 2, P], F32, name=f"bank{d + 1}")
+            for u in range(2):
+                nc.tensor.transpose(spread[:, u, :], gate_cols[:, u, d : d + 1].to_broadcast([P, P]), ident[:])
+            nc.scalar.copy(gates[:, d, :], spread[:].rearrange("p u v -> p (u v)"))
         third = keep.tile([P, 4, V], F32, name="third")
         nc.vector.memset(third[:, 0:2, :], 0.0)
 

@@ -134,6 +134,10 @@ def tile_picked_sage_silu_e_kernel(tc, xT, w1, w2, gate, offs, pos1, pos2, pos3,
         def fetch(dest, t, d):
             nc.vector.tensor_tensor(dest, h[t][:].indirect(pos_t[d][:]), gates[:, d, :], MULT)
 
+        def fetch_half(dest, t, d, u):
+            cols = slice(128 * u, 128 * u + 128)
+            nc.vector.tensor_tensor(dest[:, cols], h[t][:].indirect(pos_t[d][:, 8 * u : 8 * u + 8]), gates[:, d, cols], MULT)
+
         def flip(bank, t, d, u, last):
             nc.tensor.matmul(bank, terms[d][:, t, 128 * u : 128 * u + 128], ident[:], is_transpose=True, start=d == 0, stop=d == last)
 
@@ -144,10 +148,11 @@ def tile_picked_sage_silu_e_kernel(tc, xT, w1, w2, gate, offs, pos1, pos2, pos3,
             nc.scalar.copy(w2_out4[:, 64 * m : 64 * m + 64], w2_in4[:, 64 * m : 64 * m + 64])
 
         flat_low = w2_raw[:, :, 64:192]
+        cast_w2(0)
         for t in range(2):
             for d in range(D):
                 fetch(terms[d][:, t, :], t, d)
-            cast_w2(t)
+            cast_w2(t + 1)
             flipped = psum.tile([P, 2, 128], F32, name=f"flipped{t}")
             for u in range(2):
                 for d in range(D):
@@ -159,19 +164,19 @@ def tile_picked_sage_silu_e_kernel(tc, xT, w1, w2, gate, offs, pos1, pos2, pos3,
 
         for d in range(2):
             fetch(terms[d][:, 2, :], 2, d)
-        cast_w2(2)
         cast_w2(3)
         flipped = psum.tile([P, 2, 128], F32, name="flipped0")
         for u in range(2):
             for d in range(2):
                 flip(flipped[:, u, :], 2, d, u, 1)
-        flat = w2_raw[:, 0:2, 384:512]
+        flat = w2_raw[:, 3, 256:512].rearrange("p (u v) -> p u v", u=2)
         nc.scalar.copy(flat, flipped[:])
         for u in range(2):
             nc.tensor.transpose(parts[u][:, 2, :], flat[:, u, :], ident[:])
 
-        for d in range(2):
-            fetch(terms[d][:, 3, :], 3, d)
+        fetch(terms[0][:, 3, :], 3, 0)
+        for u in range(2):
+            fetch_half(terms[1][:, 3, :], 3, 1, u)
         halves = [psum.tile([P, 128], F32, name=tag) for tag in ("flipped1", "flipped0")]
         for d in range(2):
             for u in range(2):
@@ -180,35 +185,40 @@ def tile_picked_sage_silu_e_kernel(tc, xT, w1, w2, gate, offs, pos1, pos2, pos3,
             flat = keep.tile([P, 128], F32, align_bytes=64, name=f"flat_last{u}")
             nc.scalar.copy(flat[:], halves[u][:])
             nc.tensor.transpose(parts[u][:, 3, :], flat[:], ident[:])
-        for t in range(2, 4):
-            fetch(third[:, t, :], t, 2)
-        w2_codes = [keep.tile([P, 256], U32, align_bytes=64, name=tag) for tag in ("w2_codes", "flat_last0")]
+        fetch(third[:, 2, :], 2, 2)
+        for u in range(2):
+            fetch_half(third[:, 3, :], 3, 2, u)
+        w2_tiles = [keep.tile([P, 2 * P], U32, align_bytes=64, name=f"flat_last{u}") for u in range(2)]
+        w2_codes = [w2_tiles[m // 2][:, P * (m % 2) : P * (m % 2) + P] for m in range(4)]
 
-        def quantize_w2(a):
-            nc.vector.quantize_mx(
-                out=w2_codes[a][:].bitcast(FP8X4),
-                scales=w2_scales[:, 256 * a : 256 * a + 256],
-                in_=w2g_flat[:, 1024 * a : 1024 * a + 1024],
-            )
+        def quantize_w2(codes, a, b):
+            nc.vector.quantize_mx(out=codes.bitcast(FP8X4), scales=w2_scales[:, a:b], in_=w2g_flat[:, PACK * a : PACK * b])
 
         zg = [keep.tile([P, 128, PACK], BF16, align_bytes=64, name=f"zg{u}") for u in range(2)]
         z_codes = [keep.tile([P, 128], U32, align_bytes=64, name=f"z_codes{u}") for u in range(2)]
         z_scales = [keep.tile([P, 128], U8, align_bytes=64, name=f"z_scales{u}") for u in range(2)]
-        for u in range(2):
-            if u == 0:
-                quantize_w2(0)
+
+        def add_third(u):
             z_out = zg[u][:].rearrange("p (c i) t -> p c t i", i=2)
             z_in = parts[u][:].rearrange("p t (c i) -> p c t i", i=2)
             last_in = third[:, :, 128 * u : 128 * u + 128].rearrange("p t (c i) -> p c t i", i=2)
             nc.vector.tensor_tensor(z_out, z_in, last_in, ADD)
-            if u == 0:
-                quantize_w2(1)
+
+        def quantize_z(u):
             quantize(z_codes[u], z_scales[u], zg[u][:].rearrange("p v j -> p (v j)"), 0, 128)
+
+        add_third(0)
+        quantize_w2(w2_tiles[0][:], 0, 2 * P)
+        quantize_z(0)
+        quantize_w2(w2_codes[2], 2 * P, 3 * P)
+        add_third(1)
+        quantize_w2(w2_codes[3], 3 * P, N)
+        quantize_z(1)
 
         def layer2(bank, m, u):
             nc.tensor.matmul_mx(
                 out=bank,
-                lhsT=w2_codes[m // 2][:, 128 * (m % 2) : 128 * (m % 2) + 128].bitcast(FP8X4),
+                lhsT=w2_codes[m].bitcast(FP8X4),
                 lhsT_scale=w2_scales[:, 128 * m : 128 * m + 128],
                 rhs=z_codes[u][:].bitcast(FP8X4),
                 rhs_scale=z_scales[u][:],
@@ -217,13 +227,13 @@ def tile_picked_sage_silu_e_kernel(tc, xT, w1, w2, gate, offs, pos1, pos2, pos3,
             )
 
         out_view = out.rearrange("(m p) v -> p m v", p=P)
-        for g in range(2):
-            o_bank = psum.tile([P, 2, 128], F32, name=f"flipped{g}")
-            for i in range(2):
-                layer2(o_bank[:, i, :], 2 * g + i, 0)
-            staged = keep.tile([P, 2, 128], F32, name=f"staged{g}")
+        for g, (a, b) in enumerate(((0, 3), (3, 4))):
+            o_bank = psum.tile([P, b - a, 128], F32, name=f"flipped{g}")
+            for m in range(a, b):
+                layer2(o_bank[:, m - a, :], m, 0)
+            staged = keep.tile([P, b - a, 128], F32, name=f"staged{g}")
             nc.scalar.copy(staged[:], o_bank[:])
-            nc.sync.dma_start(out_view[:, 2 * g : 2 * g + 2, 0:128], staged[:])
+            nc.sync.dma_start(out_view[:, a:b, 0:128], staged[:])
         for m in range(4):
             o_bank = psum.tile([P, 128], F32, name=f"bank{m}")
             layer2(o_bank[:], m, 1)

@@ -129,7 +129,6 @@ def tile_picked_sage_silu_e_kernel(tc, xT, w1, w2, gate, offs, pos1, pos2, pos3,
             nc.scalar.activation(h[t][:], banks[t][:], SILU)
 
         terms = [keep.tile([P, 4 if d < 2 else 2, V], F32, name=f"term{d}") for d in range(D)]
-        parts = [psum.tile([P, 4, 128], F32, name=f"part{u}") for u in range(2)]
 
         def fetch(dest, t, d):
             nc.vector.tensor_tensor(dest, h[t][:].indirect(pos_t[d][:]), gates[:, d, :], MULT)
@@ -138,8 +137,8 @@ def tile_picked_sage_silu_e_kernel(tc, xT, w1, w2, gate, offs, pos1, pos2, pos3,
             cols = slice(128 * u, 128 * u + 128)
             nc.vector.tensor_tensor(dest[:, cols], h[t][:].indirect(pos_t[d][:, 8 * u : 8 * u + 8]), gates[:, d, cols], MULT)
 
-        def flip(bank, t, d, u, last):
-            nc.tensor.matmul(bank, terms[d][:, t, 128 * u : 128 * u + 128], ident[:], is_transpose=True, start=d == 0, stop=d == last)
+        def flip(bank, t, d, u, start, stop):
+            nc.tensor.matmul(bank, terms[d][:, t, 128 * u : 128 * u + 128], ident[:], is_transpose=True, start=start, stop=stop)
 
         w2_in4 = w2_raw[:].rearrange("p j (c i) -> p c j i", i=2)
         w2_out4 = w2g[:].rearrange("p (c i) j -> p c j i", i=2)
@@ -148,43 +147,47 @@ def tile_picked_sage_silu_e_kernel(tc, xT, w1, w2, gate, offs, pos1, pos2, pos3,
             nc.scalar.copy(w2_out4[:, 64 * m : 64 * m + 64], w2_in4[:, 64 * m : 64 * m + 64])
 
         flat_low = w2_raw[:, :, 64:192]
-        cast_w2(0)
         for t in range(2):
             for d in range(D):
                 fetch(terms[d][:, t, :], t, d)
-            cast_w2(t + 1)
+            cast_w2(t)
             flipped = psum.tile([P, 2, 128], F32, name=f"flipped{t}")
-            for u in range(2):
-                for d in range(D):
-                    flip(flipped[:, u, :], t, d, u, 2)
+            for d in range(D):
+                for u in range(2):
+                    flip(flipped[:, u, :], t, d, u, (d, u) == (0, 0), (d, u) == (2, 1))
             nc.scalar.copy(flat_low[:, :, 64 * t : 64 * t + 64], flipped[:].rearrange("p u (s m) -> p (u s) m", s=2))
-        for u in range(2):
-            for s in range(2):
-                nc.tensor.transpose(parts[u][:, s, :], flat_low[:, 2 * u + s, :], ident[:])
 
         for d in range(2):
             fetch(terms[d][:, 2, :], 2, d)
-        cast_w2(3)
+        cast_w2(2)
         flipped = psum.tile([P, 2, 128], F32, name="flipped0")
-        for u in range(2):
-            for d in range(2):
-                flip(flipped[:, u, :], 2, d, u, 1)
-        flat = w2_raw[:, 3, 256:512].rearrange("p (u v) -> p u v", u=2)
-        nc.scalar.copy(flat, flipped[:])
-        for u in range(2):
-            nc.tensor.transpose(parts[u][:, 2, :], flat[:, u, :], ident[:])
+        for d in range(2):
+            for u in range(2):
+                flip(flipped[:, u, :], 2, d, u, (d, u) == (0, 0), (d, u) == (1, 1))
+        flat_mid = keep.tile([P, 2, 128], F32, name="flat_mid")
+        nc.scalar.copy(flat_mid[:], flipped[:])
 
         fetch(terms[0][:, 3, :], 3, 0)
         for u in range(2):
             fetch_half(terms[1][:, 3, :], 3, 1, u)
-        halves = [psum.tile([P, 128], F32, name=tag) for tag in ("flipped1", "flipped0")]
-        for d in range(2):
-            for u in range(2):
-                flip(halves[u][:], 3, d, u, 1)
-        for u in range(2):
+        parts = []
+        for u, (last_tag, part_tag) in enumerate((("flipped1", "part0"), ("flipped0", "flipped1"))):
+            last = psum.tile([P, 128], F32, name=last_tag)
+            part = psum.tile([P, 4, 128], F32, name=part_tag)
+            parts.append(part)
+            if u == 0:
+                for s in range(2):
+                    nc.tensor.transpose(part[:, s, :], flat_low[:, s, :], ident[:])
+            for d in range(2):
+                flip(last[:], 3, d, u, d == 0, d == 1)
+            if u == 1:
+                for s in range(2):
+                    nc.tensor.transpose(part[:, s, :], flat_low[:, 2 + s, :], ident[:])
+            nc.tensor.transpose(part[:, 2, :], flat_mid[:, u, :], ident[:])
             flat = keep.tile([P, 128], F32, align_bytes=64, name=f"flat_last{u}")
-            nc.scalar.copy(flat[:], halves[u][:])
-            nc.tensor.transpose(parts[u][:, 3, :], flat[:], ident[:])
+            nc.scalar.copy(flat[:], last[:])
+            nc.tensor.transpose(part[:, 3, :], flat[:], ident[:])
+        cast_w2(3)
         fetch(third[:, 2, :], 2, 2)
         for u in range(2):
             fetch_half(third[:, 3, :], 3, 2, u)
@@ -228,7 +231,7 @@ def tile_picked_sage_silu_e_kernel(tc, xT, w1, w2, gate, offs, pos1, pos2, pos3,
 
         out_view = out.rearrange("(m p) v -> p m v", p=P)
         for g, (a, b) in enumerate(((0, 3), (3, 4))):
-            o_bank = psum.tile([P, b - a, 128], F32, name=f"flipped{g}")
+            o_bank = psum.tile([P, b - a, 128], F32, name=("flipped0", "part1")[g])
             for m in range(a, b):
                 layer2(o_bank[:, m - a, :], m, 0)
             staged = keep.tile([P, b - a, 128], F32, name=f"staged{g}")

@@ -31,7 +31,7 @@ def tile_picked_sage_silu_e_kernel(tc, xT, w1, w2, gate, offs, pos1, pos2, pos3,
         x_view = xT.rearrange("(p j) t -> p j t", j=PACK)
         w1_view = w1.rearrange("(p j) c -> p j c", j=PACK)
         w1_raw = [keep.tile([P, PACK, 256], F32, name=f"w1_raw{b}") for b in range(2)]
-        w2_raw = keep.tile([P, PACK, N], F32, name="w2_raw")
+        w2_raw = [keep.tile([P, PACK, 256], F32, name=f"w2_raw{b}") for b in range(2)]
         gates = keep.tile([P, D, V], F32, name="gates")
         pos_t = [keep.tile([P, V // 16], U16, name=f"pos_t{d}") for d in range(D)]
 
@@ -46,7 +46,9 @@ def tile_picked_sage_silu_e_kernel(tc, xT, w1, w2, gate, offs, pos1, pos2, pos3,
             nc.sync.dma_start(w1_raw[b][:], w1_view[:, :, 256 * b : 256 * b + 256])
         for d, pos in enumerate((pos1, pos2, pos3)):
             nc.sync.dma_start(pos_t[d][:], pos)
-        nc.sync.dma_start(w2_raw[:], w2.rearrange("(p j) m -> p j m", j=PACK))
+        w2_view = w2.rearrange("(p j) m -> p j m", j=PACK)
+        for b in range(2):
+            nc.sync.dma_start(w2_raw[b][:], w2_view[:, :, 256 * b : 256 * b + 256])
 
         warm = keep.tile([P, 1], F32, name="warm")
         warm_out = keep.tile([P, 1], F32, name="warm_out")
@@ -64,24 +66,22 @@ def tile_picked_sage_silu_e_kernel(tc, xT, w1, w2, gate, offs, pos1, pos2, pos3,
             for u in range(2):
                 nc.tensor.transpose(spread[:, u, :], gate_cols[:, u, d : d + 1].to_broadcast([P, P]), ident[:])
             nc.scalar.copy(gates[:, d, :], spread[:].rearrange("p u v -> p (u v)"))
-        third = keep.tile([P, 4, V], F32, name="third")
-        nc.vector.memset(third[:, 0:2, :], 0.0)
+        third = keep.tile([P, 2, V], F32, name="third")
 
         xg = keep.tile([P, S, PACK], BF16, align_bytes=64, name="xg")
         x_codes = keep.tile([P, S], U32, align_bytes=64, name="x_codes")
         x_scales = keep.tile([P, S], U8, align_bytes=64, name="x_scales")
-        w1g_low = [keep.tile([P, 2, 64, PACK], BF16, align_bytes=64, name=f"w1g_low{b}") for b in range(2)]
+        w1g_low = [keep.tile([P, 64, 2, PACK], BF16, align_bytes=64, name=f"w1g_low{b}") for b in range(2)]
         w1g_high = keep.tile([P, 2, P, PACK], BF16, align_bytes=64, name="w1g_high")
         w1_codes = [keep.tile([P, w], U32, align_bytes=64, name=f"w1_codes{t}") for t, w in enumerate((P, P, 2 * P))]
         w1_scales = [keep.tile([P, w], U8, align_bytes=64, name=f"w1_scales{t}") for t, w in enumerate((P, P, 2 * P))]
-        w2g = keep.tile([P, N, PACK], BF16, align_bytes=64, name="w2g")
+        w2g = keep.tile([P, 2 * P, PACK], BF16, align_bytes=64, name="w2g")
         w2_scales = keep.tile([P, N], U8, align_bytes=64, name="w2_scales")
 
         def quantize(codes, scales, grouped, a, b):
             nc.vector.quantize_mx(out=codes[:, a:b].bitcast(FP8X4), scales=scales[:, a:b], in_=grouped[:, PACK * a : PACK * b])
 
         xg_flat = xg[:].rearrange("p s j -> p (s j)")
-        w2g_flat = w2g[:].rearrange("p m j -> p (m j)")
 
         for j in range(3):
             nc.vector.tensor_copy(xg[:, :, j], planes[j][:].indirect(offs_t[:]))
@@ -93,7 +93,7 @@ def tile_picked_sage_silu_e_kernel(tc, xT, w1, w2, gate, offs, pos1, pos2, pos3,
         h = [keep.tile([P, S], F32, name=f"h{t}") for t in range(4)]
 
         def cast_low(b, copy):
-            copy(w1g_low[b][:].rearrange("p t m j -> p m j t"), w1_in[b][0])
+            copy(w1g_low[b][:].rearrange("p m t j -> p m j t"), w1_in[b][0])
 
         def cast_high(b, copy):
             copy(w1g_high[:].rearrange("p t m j -> p m j t")[:, 64 * b : 64 * b + 64], w1_in[b][1])
@@ -114,11 +114,11 @@ def tile_picked_sage_silu_e_kernel(tc, xT, w1, w2, gate, offs, pos1, pos2, pos3,
         cast_low(0, nc.scalar.copy)
         cast_high(0, nc.scalar.copy)
         quantize(x_codes, x_scales, xg_flat, 0, 256)
-        quantize(w1_codes[0], w1_scales[0], w1g_low[0][:].rearrange("p t m j -> p (t m j)"), 0, P)
+        quantize(w1_codes[0], w1_scales[0], w1g_low[0][:].rearrange("p m t j -> p (m t j)"), 0, P)
         quantize(x_codes, x_scales, xg_flat, 256, 512)
         cast_low(1, nc.vector.tensor_copy)
         cast_high(1, nc.vector.tensor_copy)
-        quantize(w1_codes[1], w1_scales[1], w1g_low[1][:].rearrange("p t m j -> p (t m j)"), 0, P)
+        quantize(w1_codes[1], w1_scales[1], w1g_low[1][:].rearrange("p m t j -> p (m t j)"), 0, P)
         quantize(w1_codes[2], w1_scales[2], w1g_high[:].rearrange("p t m j -> p (t m j)"), 0, 2 * P)
         for tag, a, b in (("part0", 0, 256), ("bank0", 256, 512)):
             bank = psum.tile([P, b - a], F32, name=tag)
@@ -128,7 +128,7 @@ def tile_picked_sage_silu_e_kernel(tc, xT, w1, w2, gate, offs, pos1, pos2, pos3,
             layer1(banks[t][:], t, slice(0, S))
             nc.scalar.activation(h[t][:], banks[t][:], SILU)
 
-        terms = [keep.tile([P, 4 if d < 2 else 2, V], F32, name=f"term{d}") for d in range(D)]
+        terms = {(t, d): keep.tile([P, V], F32, align_bytes=64, name=f"term{t}{d}") for t in range(4) for d in range(3 if t < 2 else 2)}
 
         def fetch(dest, t, d):
             nc.vector.tensor_tensor(dest, h[t][:].indirect(pos_t[d][:]), gates[:, d, :], MULT)
@@ -138,71 +138,79 @@ def tile_picked_sage_silu_e_kernel(tc, xT, w1, w2, gate, offs, pos1, pos2, pos3,
             nc.vector.tensor_tensor(dest[:, cols], h[t][:].indirect(pos_t[d][:, 8 * u : 8 * u + 8]), gates[:, d, cols], MULT)
 
         def flip(bank, t, d, u, start, stop):
-            nc.tensor.matmul(bank, terms[d][:, t, 128 * u : 128 * u + 128], ident[:], is_transpose=True, start=start, stop=stop)
+            nc.tensor.matmul(bank, terms[t, d][:, 128 * u : 128 * u + 128], ident[:], is_transpose=True, start=start, stop=stop)
 
-        w2_in4 = w2_raw[:].rearrange("p j (c i) -> p c j i", i=2)
-        w2_out4 = w2g[:].rearrange("p (c i) j -> p c j i", i=2)
+        w2_in4 = [w2_raw[b][:].rearrange("p j (c i) -> p c j i", i=2) for b in range(2)]
 
-        def cast_w2(m):
-            nc.scalar.copy(w2_out4[:, 64 * m : 64 * m + 64], w2_in4[:, 64 * m : 64 * m + 64])
+        def cast_w2(m, dest):
+            nc.scalar.copy(dest.rearrange("p (c i) j -> p c j i", i=2), w2_in4[m // 2][:, 64 * (m % 2) : 64 * (m % 2) + 64])
 
-        flat_low = w2_raw[:, :, 64:192]
+        for m in range(2):
+            cast_w2(m, w2g[:, P * m : P * m + P])
+        flat_low = keep.tile([P, 2, 128], F32, name="w2_raw0")
         for t in range(2):
             for d in range(D):
-                fetch(terms[d][:, t, :], t, d)
-            cast_w2(t)
+                fetch(terms[t, d][:], t, d)
             flipped = psum.tile([P, 2, 128], F32, name=f"flipped{t}")
             for d in range(D):
                 for u in range(2):
                     flip(flipped[:, u, :], t, d, u, (d, u) == (0, 0), (d, u) == (2, 1))
-            nc.scalar.copy(flat_low[:, :, 64 * t : 64 * t + 64], flipped[:].rearrange("p u (s m) -> p (u s) m", s=2))
+            nc.scalar.copy(flat_low[:, :, 64 * t : 64 * t + 64].bitcast(BF16), flipped[:])
+        zg = [keep.tile([P, 128, PACK], BF16, align_bytes=64, name=f"zg{u}") for u in range(2)]
+        pairs = psum.tile([P, 128], F32, name="bank1")
+        nc.tensor.transpose(pairs[:], flat_low[:, 0, :], ident[:])
+
+        def place_pairs(u, source):
+            words = zg[u][:].rearrange("p v j -> p (v j)").bitcast(F32).rearrange("p (v w) -> p v w", w=2)
+            nc.scalar.copy(words[:, :, 0], source)
+
+        place_pairs(0, pairs[:])
 
         for d in range(2):
-            fetch(terms[d][:, 2, :], 2, d)
-        cast_w2(2)
+            fetch(terms[2, d][:], 2, d)
         flipped = psum.tile([P, 2, 128], F32, name="flipped0")
         for d in range(2):
             for u in range(2):
                 flip(flipped[:, u, :], 2, d, u, (d, u) == (0, 0), (d, u) == (1, 1))
+        w2g_late = [keep.tile([P, P, PACK], BF16, align_bytes=64, name="w2g_third")]
+        cast_w2(2, w2g_late[0][:])
         flat_mid = keep.tile([P, 2, 128], F32, name="flat_mid")
         nc.scalar.copy(flat_mid[:], flipped[:])
 
-        fetch(terms[0][:, 3, :], 3, 0)
+
+        fetch(terms[3, 0][:], 3, 0)
         for u in range(2):
-            fetch_half(terms[1][:, 3, :], 3, 1, u)
+            fetch_half(terms[3, 1][:], 3, 1, u)
         parts = []
         for u, (last_tag, part_tag) in enumerate((("flipped1", "part0"), ("flipped0", "flipped1"))):
-            last = psum.tile([P, 128], F32, name=last_tag)
-            part = psum.tile([P, 4, 128], F32, name=part_tag)
+            last = psum.tile([P, 2, 128], F32, name=last_tag)
+            part = psum.tile([P, 2, 128], F32, name=part_tag)
             parts.append(part)
-            if u == 0:
-                for s in range(2):
-                    nc.tensor.transpose(part[:, s, :], flat_low[:, s, :], ident[:])
-            for d in range(2):
-                flip(last[:], 3, d, u, d == 0, d == 1)
             if u == 1:
-                for s in range(2):
-                    nc.tensor.transpose(part[:, s, :], flat_low[:, 2 + s, :], ident[:])
-            nc.tensor.transpose(part[:, 2, :], flat_mid[:, u, :], ident[:])
+                nc.tensor.transpose(last[:, 1, :], flat_low[:, u, :], ident[:])
+            for d in range(2):
+                flip(last[:, 0, :], 3, d, u, d == 0, d == 1)
+            nc.tensor.transpose(part[:, 0, :], flat_mid[:, u, :], ident[:])
             flat = keep.tile([P, 128], F32, align_bytes=64, name=f"flat_last{u}")
-            nc.scalar.copy(flat[:], last[:])
-            nc.tensor.transpose(part[:, 3, :], flat[:], ident[:])
-        cast_w2(3)
-        fetch(third[:, 2, :], 2, 2)
+            nc.scalar.copy(flat[:], last[:, 0, :])
+            nc.tensor.transpose(part[:, 1, :], flat[:], ident[:])
+        place_pairs(1, last[:, 1, :])
+        w2g_late.append(keep.tile([P, P, PACK], BF16, align_bytes=64, name="term31"))
+        cast_w2(3, w2g_late[1][:])
+        fetch(third[:, 0, :], 2, 2)
         for u in range(2):
-            fetch_half(third[:, 3, :], 3, 2, u)
+            fetch_half(third[:, 1, :], 3, 2, u)
         w2_tiles = [keep.tile([P, 2 * P], U32, align_bytes=64, name=f"flat_last{u}") for u in range(2)]
         w2_codes = [w2_tiles[m // 2][:, P * (m % 2) : P * (m % 2) + P] for m in range(4)]
 
-        def quantize_w2(codes, a, b):
-            nc.vector.quantize_mx(out=codes.bitcast(FP8X4), scales=w2_scales[:, a:b], in_=w2g_flat[:, PACK * a : PACK * b])
+        def quantize_w2(codes, a, b, grouped):
+            nc.vector.quantize_mx(out=codes.bitcast(FP8X4), scales=w2_scales[:, a:b], in_=grouped[:].rearrange("p m j -> p (m j)"))
 
-        zg = [keep.tile([P, 128, PACK], BF16, align_bytes=64, name=f"zg{u}") for u in range(2)]
         z_codes = [keep.tile([P, 128], U32, align_bytes=64, name=f"z_codes{u}") for u in range(2)]
         z_scales = [keep.tile([P, 128], U8, align_bytes=64, name=f"z_scales{u}") for u in range(2)]
 
         def add_third(u):
-            z_out = zg[u][:].rearrange("p (c i) t -> p c t i", i=2)
+            z_out = zg[u][:, :, 2:4].rearrange("p (c i) t -> p c t i", i=2)
             z_in = parts[u][:].rearrange("p t (c i) -> p c t i", i=2)
             last_in = third[:, :, 128 * u : 128 * u + 128].rearrange("p t (c i) -> p c t i", i=2)
             nc.vector.tensor_tensor(z_out, z_in, last_in, ADD)
@@ -211,11 +219,11 @@ def tile_picked_sage_silu_e_kernel(tc, xT, w1, w2, gate, offs, pos1, pos2, pos3,
             quantize(z_codes[u], z_scales[u], zg[u][:].rearrange("p v j -> p (v j)"), 0, 128)
 
         add_third(0)
-        quantize_w2(w2_tiles[0][:], 0, 2 * P)
+        quantize_w2(w2_tiles[0][:], 0, 2 * P, w2g)
         quantize_z(0)
-        quantize_w2(w2_codes[2], 2 * P, 3 * P)
+        quantize_w2(w2_codes[2], 2 * P, 3 * P, w2g_late[0])
         add_third(1)
-        quantize_w2(w2_codes[3], 3 * P, N)
+        quantize_w2(w2_codes[3], 3 * P, N, w2g_late[1])
         quantize_z(1)
 
         def layer2(bank, m, u):
@@ -230,8 +238,8 @@ def tile_picked_sage_silu_e_kernel(tc, xT, w1, w2, gate, offs, pos1, pos2, pos3,
             )
 
         out_view = out.rearrange("(m p) v -> p m v", p=P)
-        for g, (a, b) in enumerate(((0, 3), (3, 4))):
-            o_bank = psum.tile([P, b - a, 128], F32, name=("flipped0", "part1")[g])
+        for g, (a, b) in enumerate(((0, 2), (2, 3), (3, 4))):
+            o_bank = psum.tile([P, b - a, 128], F32, name=("part1", "part0", "flipped0")[g])
             for m in range(a, b):
                 layer2(o_bank[:, m - a, :], m, 0)
             staged = keep.tile([P, b - a, 128], F32, name=f"staged{g}")

@@ -178,9 +178,9 @@ def tile_picked_sage_silu_e_kernel(tc, xT, w1, w2, gate, offs, pos1, pos2, pos3,
         nc.scalar.copy(flat_mid[:], flipped[:])
 
 
-        fetch(terms[3, 0][:], 3, 0)
         for u in range(2):
-            fetch_half(terms[3, 1][:], 3, 1, u)
+            for d in range(2):
+                fetch_half(terms[3, d][:], 3, d, u)
         parts = []
         for u, (last_tag, part_tag) in enumerate((("flipped1", "part0"), ("flipped0", "flipped1"))):
             last = psum.tile([P, 2, 128], F32, name=last_tag)

@@ -14,10 +14,12 @@ FP8X4 = mybir.dt.float8_e4m3fn_x4
 MULT = mybir.AluOpType.mult
 ADD = mybir.AluOpType.add
 SILU = mybir.ActivationFunctionType.Silu
+COPY = mybir.ActivationFunctionType.Copy
 
 P = 128
 K, T, S, V, H, N, D = 512, 2048, 512, 256, 512, 512, 3
 PACK = 4
+HALF = 256
 
 
 def tile_picked_sage_silu_e_kernel(tc, xT, w1, w2, gate, offs, pos1, pos2, pos3, out):
@@ -27,15 +29,15 @@ def tile_picked_sage_silu_e_kernel(tc, xT, w1, w2, gate, offs, pos1, pos2, pos3,
         psum = ctx.enter_context(tc.psum_pool(name="psum", bufs=1))
 
         offs_t = keep.tile([P, S // 16], U16, name="offs_t")
+        pos_t = [keep.tile([P, V // 16], U16, name=f"pos_t{d}") for d in range(D)]
         planes = [keep.tile([P, T], F32, name=f"plane{j}") for j in range(PACK)]
+        w1_raw = [keep.tile([P, PACK, HALF], F32, name=f"w1_raw{b}") for b in range(2)]
+        w2_raw = [keep.tile([P, PACK, HALF], F32, name=f"w2_raw{b}") for b in range(2)]
+        gate_rows = keep.tile([P, V], F32, name="gate_rows")
         x_view = xT.rearrange("(p j) t -> p j t", j=PACK)
         w1_view = w1.rearrange("(p j) c -> p j c", j=PACK)
-        w1_raw = [keep.tile([P, PACK, 256], F32, name=f"w1_raw{b}") for b in range(2)]
-        w2_raw = [keep.tile([P, PACK, 256], F32, name=f"w2_raw{b}") for b in range(2)]
-        gates = keep.tile([P, D, V], F32, name="gates")
-        pos_t = [keep.tile([P, V // 16], U16, name=f"pos_t{d}") for d in range(D)]
+        w2_view = w2.rearrange("(p j) m -> p j m", j=PACK)
 
-        gate_rows = keep.tile([P, V], F32, name="gate_rows")
         nc.gpsimd.memset(gate_rows[:], 0.0)
         for j in range(PACK):
             nc.sync.dma_start(planes[j][:], x_view[:, j, :])
@@ -43,30 +45,30 @@ def tile_picked_sage_silu_e_kernel(tc, xT, w1, w2, gate, offs, pos1, pos2, pos3,
                 nc.sync.dma_start(gate_rows[0:D, :], gate[:, 0, :])
                 nc.sync.dma_start(offs_t[:], offs)
         for b in range(2):
-            nc.sync.dma_start(w1_raw[b][:], w1_view[:, :, 256 * b : 256 * b + 256])
+            nc.sync.dma_start(w1_raw[b][:], w1_view[:, :, HALF * b : HALF * b + HALF])
         for d, pos in enumerate((pos1, pos2, pos3)):
             nc.sync.dma_start(pos_t[d][:], pos)
-        w2_view = w2.rearrange("(p j) m -> p j m", j=PACK)
         for b in range(2):
-            nc.sync.dma_start(w2_raw[b][:], w2_view[:, :, 256 * b : 256 * b + 256])
+            nc.sync.dma_start(w2_raw[b][:], w2_view[:, :, HALF * b : HALF * b + HALF])
 
         warm = keep.tile([P, 1], F32, name="warm")
         warm_out = keep.tile([P, 1], F32, name="warm_out")
         nc.vector.memset(warm[:], 0.0)
         nc.scalar.activation(warm_out[:], warm[:], SILU)
+
         ident = keep.tile([P, P], F32, name="ident")
         make_identity(nc, ident[:])
-        turned = psum.tile([P, 2, P], F32, name="bank1")
+        turned = psum.tile([P, 2, P], F32, name="bank2")
         for u in range(2):
             nc.tensor.transpose(turned[:, u, :], gate_rows[:, P * u : P * u + P], ident[:])
         gate_cols = keep.tile([P, 2, D], F32, name="gate_cols")
         nc.scalar.copy(gate_cols[:], turned[:, :, 0:D])
+        gates = keep.tile([P, D, V], F32, name="gates")
         for d in range(D):
-            spread = psum.tile([P, 2, P], F32, name=f"bank{d + 1}")
+            spread = psum.tile([P, 2, P], F32, name=f"bank{d + 2}")
             for u in range(2):
                 nc.tensor.transpose(spread[:, u, :], gate_cols[:, u, d : d + 1].to_broadcast([P, P]), ident[:])
             nc.scalar.copy(gates[:, d, :], spread[:].rearrange("p u v -> p (u v)"))
-        third = keep.tile([P, 2, V], F32, name="third")
 
         xg = keep.tile([P, S, PACK], BF16, align_bytes=64, name="xg")
         x_codes = keep.tile([P, S], U32, align_bytes=64, name="x_codes")
@@ -75,22 +77,27 @@ def tile_picked_sage_silu_e_kernel(tc, xT, w1, w2, gate, offs, pos1, pos2, pos3,
         w1g_high = keep.tile([P, 2, P, PACK], BF16, align_bytes=64, name="w1g_high")
         w1_codes = [keep.tile([P, w], U32, align_bytes=64, name=f"w1_codes{t}") for t, w in enumerate((P, P, 2 * P))]
         w1_scales = [keep.tile([P, w], U8, align_bytes=64, name=f"w1_scales{t}") for t, w in enumerate((P, P, 2 * P))]
-        w2g = keep.tile([P, 2 * P, PACK], BF16, align_bytes=64, name="w2g")
-        w2_scales = keep.tile([P, N], U8, align_bytes=64, name="w2_scales")
 
-        def quantize(codes, scales, grouped, a, b):
-            nc.vector.quantize_mx(out=codes[:, a:b].bitcast(FP8X4), scales=scales[:, a:b], in_=grouped[:, PACK * a : PACK * b])
+        def quantize(codes, scales, grouped):
+            nc.vector.quantize_mx(out=codes.bitcast(FP8X4), scales=scales, in_=grouped)
 
-        xg_flat = xg[:].rearrange("p s j -> p (s j)")
+        def multiply(bank, lhs_codes, lhs_scales, rhs_codes, rhs_scales):
+            nc.tensor.matmul_mx(
+                out=bank,
+                lhsT=lhs_codes.bitcast(FP8X4),
+                lhsT_scale=lhs_scales,
+                rhs=rhs_codes.bitcast(FP8X4),
+                rhs_scale=rhs_scales,
+                start=True,
+                stop=True,
+            )
 
-        for j in range(3):
+        for j in range(PACK - 1):
             nc.vector.tensor_copy(xg[:, :, j], planes[j][:].indirect(offs_t[:]))
-        for u in range(2):
-            nc.vector.tensor_copy(xg[:, 256 * u : 256 * u + 256, 3], planes[3][:].indirect(offs_t[:, 16 * u : 16 * u + 16]))
+        for a in range(2):
+            nc.vector.tensor_copy(xg[:, HALF * a : HALF * a + HALF, 3], planes[3][:].indirect(offs_t[:, 16 * a : 16 * a + 16]))
 
         w1_in = [w1_raw[b][:].rearrange("p j (m a t) -> a p m j t", a=2, t=2) for b in range(2)]
-        banks = {t: psum.tile([P, S], F32, name=f"bank{t}") for t in range(1, 4)}
-        h = [keep.tile([P, S], F32, name=f"h{t}") for t in range(4)]
 
         def cast_low(b, copy):
             copy(w1g_low[b][:].rearrange("p m t j -> p m j t"), w1_in[b][0])
@@ -98,158 +105,141 @@ def tile_picked_sage_silu_e_kernel(tc, xT, w1, w2, gate, offs, pos1, pos2, pos3,
         def cast_high(b, copy):
             copy(w1g_high[:].rearrange("p t m j -> p m j t")[:, 64 * b : 64 * b + 64], w1_in[b][1])
 
-        def layer1(bank, t, cols):
-            w = min(t, 2)
-            c = slice(P * (t - w), P * (t - w) + P)
-            nc.tensor.matmul_mx(
-                out=bank,
-                lhsT=w1_codes[w][:, c].bitcast(FP8X4),
-                lhsT_scale=w1_scales[w][:, c],
-                rhs=x_codes[:, cols].bitcast(FP8X4),
-                rhs_scale=x_scales[:, cols],
-                start=True,
-                stop=True,
-            )
+        def quantize_x(a):
+            cols = slice(HALF * a, HALF * a + HALF)
+            quantize(x_codes[:, cols], x_scales[:, cols], xg[:, cols, :].rearrange("p s j -> p (s j)"))
+
+        def quantize_low(b):
+            quantize(w1_codes[b][:], w1_scales[b][:], w1g_low[b][:].rearrange("p m t j -> p (m t j)"))
 
         cast_low(0, nc.scalar.copy)
         cast_high(0, nc.scalar.copy)
-        quantize(x_codes, x_scales, xg_flat, 0, 256)
-        quantize(w1_codes[0], w1_scales[0], w1g_low[0][:].rearrange("p m t j -> p (m t j)"), 0, P)
-        quantize(x_codes, x_scales, xg_flat, 256, 512)
+        quantize_x(0)
+        quantize_low(0)
+        quantize_x(1)
         cast_low(1, nc.vector.tensor_copy)
         cast_high(1, nc.vector.tensor_copy)
-        quantize(w1_codes[1], w1_scales[1], w1g_low[1][:].rearrange("p m t j -> p (m t j)"), 0, P)
-        quantize(w1_codes[2], w1_scales[2], w1g_high[:].rearrange("p t m j -> p (t m j)"), 0, 2 * P)
-        for tag, a, b in (("part0", 0, 256), ("bank0", 256, 512)):
-            bank = psum.tile([P, b - a], F32, name=tag)
-            layer1(bank[:], 0, slice(a, b))
-            nc.scalar.activation(h[0][:, a:b], bank[:], SILU)
-        for t in range(1, 4):
-            layer1(banks[t][:], t, slice(0, S))
-            nc.scalar.activation(h[t][:], banks[t][:], SILU)
+        quantize_low(1)
+        quantize(w1_codes[2][:], w1_scales[2][:], w1g_high[:].rearrange("p t m j -> p (t m j)"))
 
-        terms = {(t, d): keep.tile([P, V], F32, align_bytes=64, name=f"term{t}{d}") for t in range(4) for d in range(3 if t < 2 else 2)}
+        h = [keep.tile([P, S], F32, align_bytes=64, name=f"h{t}") for t in range(PACK)]
 
-        def fetch(dest, t, d):
+        def layer1(tag, t, cols):
+            w = min(t, 2)
+            chans = slice(P * (t - w), P * (t - w) + P)
+            bank = psum.tile([P, cols.stop - cols.start], F32, name=tag)
+            multiply(bank[:], w1_codes[w][:, chans], w1_scales[w][:, chans], x_codes[:, cols], x_scales[:, cols])
+            nc.scalar.activation(h[t][:, cols], bank[:], SILU)
+
+        for a in range(2):
+            layer1(f"bank{a}", 0, slice(HALF * a, HALF * a + HALF))
+        for t in range(1, PACK):
+            layer1(f"bank{t + 1}", t, slice(0, S))
+
+        def flip(bank, source, start=True, stop=True):
+            nc.tensor.matmul(bank, source, ident[:], is_transpose=True, start=start, stop=stop)
+
+        def fetch_gated(dest, t, d):
             nc.vector.tensor_tensor(dest, h[t][:].indirect(pos_t[d][:]), gates[:, d, :], MULT)
 
-        def fetch_half(dest, t, d, u):
-            cols = slice(128 * u, 128 * u + 128)
-            nc.vector.tensor_tensor(dest[:, cols], h[t][:].indirect(pos_t[d][:, 8 * u : 8 * u + 8]), gates[:, d, cols], MULT)
+        low_sums = psum.tile([P, 2, 2, P], F32, name="bank3")
+        plain_flipped = [psum.tile([P, 2, 2, P], F32, name=f"bank{5 + d}") for d in range(2)]
 
-        def flip(bank, t, d, u, start, stop):
-            nc.tensor.matmul(bank, terms[t, d][:, 128 * u : 128 * u + 128], ident[:], is_transpose=True, start=start, stop=stop)
-
-        w2_in4 = [w2_raw[b][:].rearrange("p j (c i) -> p c j i", i=2) for b in range(2)]
-
-        def cast_w2(m, dest):
-            nc.scalar.copy(dest.rearrange("p (c i) j -> p c j i", i=2), w2_in4[m // 2][:, 64 * (m % 2) : 64 * (m % 2) + 64])
-
-        for m in range(2):
-            cast_w2(m, w2g[:, P * m : P * m + P])
-        flat_low = keep.tile([P, 2, 128], F32, name="w2_raw0")
-        for t in range(2):
-            for d in range(D):
-                fetch(terms[t, d][:], t, d)
-            flipped = psum.tile([P, 2, 128], F32, name=f"flipped{t}")
-            for d in range(D):
-                for u in range(2):
-                    flip(flipped[:, u, :], t, d, u, (d, u) == (0, 0), (d, u) == (2, 1))
-            nc.scalar.copy(flat_low[:, :, 64 * t : 64 * t + 64].bitcast(BF16), flipped[:])
-        zg = [keep.tile([P, 128, PACK], BF16, align_bytes=64, name=f"zg{u}") for u in range(2)]
-        pairs = psum.tile([P, 128], F32, name="bank1")
-        nc.tensor.transpose(pairs[:], flat_low[:, 0, :], ident[:])
-
-        def place_pairs(u, source):
-            words = zg[u][:].rearrange("p v j -> p (v j)").bitcast(F32).rearrange("p (v w) -> p v w", w=2)
-            nc.scalar.copy(words[:, :, 0], source)
-
-        place_pairs(0, pairs[:])
-
-        for d in range(2):
-            fetch(terms[2, d][:], 2, d)
-        flipped = psum.tile([P, 2, 128], F32, name="flipped0")
-        for d in range(2):
+        def low_term(b, d):
+            term = keep.tile([P, V], F32, name=f"term{b}{d}")
+            fetch_gated(term[:], b, d)
             for u in range(2):
-                flip(flipped[:, u, :], 2, d, u, (d, u) == (0, 0), (d, u) == (1, 1))
-        w2g_late = [keep.tile([P, P, PACK], BF16, align_bytes=64, name="w2g_third")]
-        cast_w2(2, w2g_late[0][:])
-        flat_mid = keep.tile([P, 2, 128], F32, name="flat_mid")
-        nc.scalar.copy(flat_mid[:], flipped[:])
+                flip(low_sums[:, u, b, :], term[:, P * u : P * u + P], (b, d, u) == (0, 0, 0), (b, d, u) == (1, 2, 1))
 
+        def high_term(t, d):
+            term = keep.tile([P, V], F32, name=f"plain{t}{d}")
+            nc.scalar.activation(term[:], h[2 + t][:].indirect(pos_t[d][:]), COPY)
+            for u in range(2):
+                flip(plain_flipped[d][:, u, t, :], term[:, P * u : P * u + P])
+
+        for d in range(D):
+            low_term(0, d)
+        high_term(0, 0)
+        low_term(1, 0)
+        high_term(1, 0)
+        low_term(1, 1)
+        high_term(0, 1)
+        low_term(1, 2)
+        high_term(1, 1)
+
+        parts = [psum.tile([P, 2, P], F32, name=f"bank{u}") for u in range(2)]
+
+        def weigh(d, u):
+            weighed = keep.tile([P, 2, P], F32, name=f"weighed{d}{u}")
+            nc.scalar.activation(weighed[:], plain_flipped[d][:, u], COPY, scale=gate_cols[:, u, d : d + 1])
+            for t in range(2):
+                flip(parts[u][:, t, :], weighed[:, t, :], (d, t) == (0, 0), (d, t) == (1, 1))
 
         for u in range(2):
-            for d in range(2):
-                fetch_half(terms[3, d][:], 3, d, u)
-        parts = []
-        for u, (last_tag, part_tag) in enumerate((("flipped1", "part0"), ("flipped0", "flipped1"))):
-            last = psum.tile([P, 2, 128], F32, name=last_tag)
-            part = psum.tile([P, 2, 128], F32, name=part_tag)
-            parts.append(part)
-            if u == 1:
-                nc.tensor.transpose(last[:, 1, :], flat_low[:, u, :], ident[:])
-            for d in range(2):
-                flip(last[:, 0, :], 3, d, u, d == 0, d == 1)
-            nc.tensor.transpose(part[:, 0, :], flat_mid[:, u, :], ident[:])
-            flat = keep.tile([P, 128], F32, align_bytes=64, name=f"flat_last{u}")
-            nc.scalar.copy(flat[:], last[:, 0, :])
-            nc.tensor.transpose(part[:, 1, :], flat[:], ident[:])
-        place_pairs(1, last[:, 1, :])
-        w2g_late.append(keep.tile([P, P, PACK], BF16, align_bytes=64, name="term31"))
-        cast_w2(3, w2g_late[1][:])
-        fetch(third[:, 0, :], 2, 2)
+            weigh(0, u)
+        low_pairs = keep.tile([P, 2, P], F32, name="low_pairs")
+        nc.scalar.copy(low_pairs[:].rearrange("p u w -> p (u w)").bitcast(BF16), low_sums[:].rearrange("p u b c -> p (u b c)"))
+        pairs = psum.tile([P, 2, P], F32, name="bank7")
         for u in range(2):
-            fetch_half(third[:, 1, :], 3, 2, u)
-        w2_tiles = [keep.tile([P, 2 * P], U32, align_bytes=64, name=f"flat_last{u}") for u in range(2)]
-        w2_codes = [w2_tiles[m // 2][:, P * (m % 2) : P * (m % 2) + P] for m in range(4)]
+            flip(pairs[:, u, :], low_pairs[:, u, :])
+        for u in range(2):
+            weigh(1, u)
+        zg = [keep.tile([P, P, PACK], BF16, align_bytes=64, name=f"zg{u}") for u in range(2)]
+        for u in range(2):
+            words = zg[u][:].rearrange("p v j -> p (v j)").bitcast(F32).rearrange("p (v w) -> p v w", w=2)
+            nc.scalar.copy(words[:, :, 0], pairs[:, u, :])
 
-        def quantize_w2(codes, a, b, grouped):
-            nc.vector.quantize_mx(out=codes.bitcast(FP8X4), scales=w2_scales[:, a:b], in_=grouped[:].rearrange("p m j -> p (m j)"))
+        third = keep.tile([P, 2, V], F32, name="third")
+        w2g = []
+        for b in range(2):
+            fetch_gated(third[:, b, :], 2 + b, 2)
+            grouped = keep.tile([P, HALF, PACK], BF16, align_bytes=64, name=f"h{2 + b}")
+            nc.vector.tensor_copy(grouped[:].rearrange("p (c i) j -> p c j i", i=2), w2_raw[b][:].rearrange("p j (c i) -> p c j i", i=2))
+            w2g.append(grouped)
+        w2_codes = keep.tile([P, N], U32, align_bytes=64, name="w2_codes")
+        w2_scales = keep.tile([P, N], U8, align_bytes=64, name="w2_scales")
 
-        z_codes = [keep.tile([P, 128], U32, align_bytes=64, name=f"z_codes{u}") for u in range(2)]
-        z_scales = [keep.tile([P, 128], U8, align_bytes=64, name=f"z_scales{u}") for u in range(2)]
+        def quantize_w2(a, b):
+            grouped = w2g[a // HALF][:, a % HALF : a % HALF + b - a, :]
+            quantize(w2_codes[:, a:b], w2_scales[:, a:b], grouped.rearrange("p m j -> p (m j)"))
+
+        z_codes = [keep.tile([P, P], U32, align_bytes=64, name=f"z_codes{u}") for u in range(2)]
+        z_scales = [keep.tile([P, P], U8, align_bytes=64, name=f"z_scales{u}") for u in range(2)]
 
         def add_third(u):
             z_out = zg[u][:, :, 2:4].rearrange("p (c i) t -> p c t i", i=2)
             z_in = parts[u][:].rearrange("p t (c i) -> p c t i", i=2)
-            last_in = third[:, :, 128 * u : 128 * u + 128].rearrange("p t (c i) -> p c t i", i=2)
+            last_in = third[:, :, P * u : P * u + P].rearrange("p t (c i) -> p c t i", i=2)
             nc.vector.tensor_tensor(z_out, z_in, last_in, ADD)
 
         def quantize_z(u):
-            quantize(z_codes[u], z_scales[u], zg[u][:].rearrange("p v j -> p (v j)"), 0, 128)
+            quantize(z_codes[u][:], z_scales[u][:], zg[u][:].rearrange("p v j -> p (v j)"))
 
+        quantize_w2(0, 256)
         add_third(0)
-        quantize_w2(w2_tiles[0][:], 0, 2 * P, w2g)
+        quantize_w2(256, 384)
         quantize_z(0)
-        quantize_w2(w2_codes[2], 2 * P, 3 * P, w2g_late[0])
         add_third(1)
-        quantize_w2(w2_codes[3], 3 * P, N, w2g_late[1])
+        quantize_w2(384, 512)
         quantize_z(1)
 
         def layer2(bank, m, u):
-            nc.tensor.matmul_mx(
-                out=bank,
-                lhsT=w2_codes[m].bitcast(FP8X4),
-                lhsT_scale=w2_scales[:, 128 * m : 128 * m + 128],
-                rhs=z_codes[u][:].bitcast(FP8X4),
-                rhs_scale=z_scales[u][:],
-                start=True,
-                stop=True,
-            )
+            cols = slice(P * m, P * m + P)
+            multiply(bank, w2_codes[:, cols], w2_scales[:, cols], z_codes[u][:], z_scales[u][:])
 
         out_view = out.rearrange("(m p) v -> p m v", p=P)
         for g, (a, b) in enumerate(((0, 2), (2, 3), (3, 4))):
-            o_bank = psum.tile([P, b - a, 128], F32, name=("part1", "part0", "flipped0")[g])
+            o_bank = psum.tile([P, b - a, P], F32, name=("bank2", "bank4", "bank3")[g])
             for m in range(a, b):
                 layer2(o_bank[:, m - a, :], m, 0)
-            staged = keep.tile([P, b - a, 128], F32, name=f"staged{g}")
+            staged = keep.tile([P, b - a, P], F32, name=f"staged{g}")
             nc.scalar.copy(staged[:], o_bank[:])
-            nc.sync.dma_start(out_view[:, a:b, 0:128], staged[:])
+            nc.sync.dma_start(out_view[:, a:b, 0:P], staged[:])
         for m in range(4):
-            o_bank = psum.tile([P, 128], F32, name=f"bank{m}")
+            o_bank = psum.tile([P, P], F32, name=("bank5", "bank6", "bank0", "bank7")[m])
             layer2(o_bank[:], m, 1)
-            staged = keep.tile([P, 128], F32, name=f"staged_last{m}")
+            staged = keep.tile([P, P], F32, name=f"staged_last{m}")
             copy = (nc.vector.tensor_copy, nc.scalar.copy)[m % 2]
             copy(staged[:], o_bank[:])
             queue = nc.scalar if m == 3 else nc.sync
-            queue.dma_start(out_view[:, m, 128:256], staged[:])
+            queue.dma_start(out_view[:, m, P : 2 * P], staged[:])

@@ -170,7 +170,7 @@ def tile_picked_sage_silu_e_kernel(tc, xT, w1, w2, gate, offs, pos1, pos2, pos3,
         parts = [psum.tile([P, 2, P], F32, name=f"bank{u}") for u in range(2)]
 
         def weigh(d, u):
-            weighed = keep.tile([P, 2, P], F32, name=f"weighed{d}{u}")
+            weighed = keep.tile([P, 2, P], F32, align_bytes=64, name=f"weighed{d}{u}")
             nc.scalar.activation(weighed[:], plain_flipped[d][:, u], COPY, scale=gate_cols[:, u, d : d + 1])
             for t in range(2):
                 flip(parts[u][:, t, :], weighed[:, t, :], (d, t) == (0, 0), (d, t) == (1, 1))
@@ -190,18 +190,24 @@ def tile_picked_sage_silu_e_kernel(tc, xT, w1, w2, gate, offs, pos1, pos2, pos3,
             nc.scalar.copy(words[:, :, 0], pairs[:, u, :])
 
         third = keep.tile([P, 2, V], F32, name="third")
-        w2g = []
-        for b in range(2):
-            fetch_gated(third[:, b, :], 2 + b, 2)
-            grouped = keep.tile([P, HALF, PACK], BF16, align_bytes=64, name=f"h{2 + b}")
-            nc.vector.tensor_copy(grouped[:].rearrange("p (c i) j -> p c j i", i=2), w2_raw[b][:].rearrange("p j (c i) -> p c j i", i=2))
-            w2g.append(grouped)
+        w2g = {}
+
+        def cast_w2(a, b, tag, copy):
+            grouped = keep.tile([P, b - a, PACK], BF16, align_bytes=64, name=tag)
+            source = w2_raw[a // HALF][:, :, a % HALF : a % HALF + b - a]
+            copy(grouped[:].rearrange("p (c i) j -> p c j i", i=2), source.rearrange("p j (c i) -> p c j i", i=2))
+            w2g[a] = grouped
+
+        cast_w2(384, 512, "weighed11", nc.scalar.copy)
+        fetch_gated(third[:, 0, :], 2, 2)
+        cast_w2(0, 256, "h2", nc.vector.tensor_copy)
+        fetch_gated(third[:, 1, :], 3, 2)
+        cast_w2(256, 384, "h3", nc.vector.tensor_copy)
         w2_codes = keep.tile([P, N], U32, align_bytes=64, name="w2_codes")
         w2_scales = keep.tile([P, N], U8, align_bytes=64, name="w2_scales")
 
         def quantize_w2(a, b):
-            grouped = w2g[a // HALF][:, a % HALF : a % HALF + b - a, :]
-            quantize(w2_codes[:, a:b], w2_scales[:, a:b], grouped.rearrange("p m j -> p (m j)"))
+            quantize(w2_codes[:, a:b], w2_scales[:, a:b], w2g[a][:].rearrange("p m j -> p (m j)"))
 
         z_codes = [keep.tile([P, P], U32, align_bytes=64, name=f"z_codes{u}") for u in range(2)]
         z_scales = [keep.tile([P, P], U8, align_bytes=64, name=f"z_scales{u}") for u in range(2)]
@@ -215,31 +221,26 @@ def tile_picked_sage_silu_e_kernel(tc, xT, w1, w2, gate, offs, pos1, pos2, pos3,
         def quantize_z(u):
             quantize(z_codes[u][:], z_scales[u][:], zg[u][:].rearrange("p v j -> p (v j)"))
 
-        quantize_w2(0, 256)
         add_third(0)
-        quantize_w2(256, 384)
+        quantize_w2(0, 256)
         quantize_z(0)
         add_third(1)
-        quantize_w2(384, 512)
+        quantize_w2(256, 384)
         quantize_z(1)
+        quantize_w2(384, 512)
 
         def layer2(bank, m, u):
             cols = slice(P * m, P * m + P)
             multiply(bank, w2_codes[:, cols], w2_scales[:, cols], z_codes[u][:], z_scales[u][:])
 
         out_view = out.rearrange("(m p) v -> p m v", p=P)
-        for g, (a, b) in enumerate(((0, 2), (2, 3), (3, 4))):
-            o_bank = psum.tile([P, b - a, P], F32, name=("bank2", "bank4", "bank3")[g])
+        pieces = ((0, 2, 0), (2, 3, 0), (0, 1, 1), (1, 2, 1), (2, 3, 1), (3, 4, 0), (3, 4, 1))
+        for g, (a, b, u) in enumerate(pieces):
+            o_bank = psum.tile([P, b - a, P], F32, name=("bank2", "bank4", "bank3", "bank5", "bank6", "bank0", "bank7")[g])
             for m in range(a, b):
-                layer2(o_bank[:, m - a, :], m, 0)
+                layer2(o_bank[:, m - a, :], m, u)
             staged = keep.tile([P, b - a, P], F32, name=f"staged{g}")
-            nc.scalar.copy(staged[:], o_bank[:])
-            nc.sync.dma_start(out_view[:, a:b, 0:P], staged[:])
-        for m in range(4):
-            o_bank = psum.tile([P, P], F32, name=("bank5", "bank6", "bank0", "bank7")[m])
-            layer2(o_bank[:], m, 1)
-            staged = keep.tile([P, P], F32, name=f"staged_last{m}")
-            copy = (nc.vector.tensor_copy, nc.scalar.copy)[m % 2]
+            copy = nc.vector.tensor_copy if g in (3, 5) else nc.scalar.copy
             copy(staged[:], o_bank[:])
-            queue = nc.scalar if m == 3 else nc.sync
-            queue.dma_start(out_view[:, m, P : 2 * P], staged[:])
+            queue = nc.scalar if g == 6 else nc.sync
+            queue.dma_start(out_view[:, a:b, P * u : P * u + P], staged[:])

@@ -234,13 +234,15 @@ def tile_picked_sage_silu_e_kernel(tc, xT, w1, w2, gate, offs, pos1, pos2, pos3,
             multiply(bank, w2_codes[:, cols], w2_scales[:, cols], z_codes[u][:], z_scales[u][:])
 
         out_view = out.rearrange("(m p) v -> p m v", p=P)
-        pieces = ((0, 2, 0), (2, 3, 0), (0, 1, 1), (1, 2, 1), (2, 3, 1), (3, 4, 0), (3, 4, 1))
-        for g, (a, b, u) in enumerate(pieces):
-            o_bank = psum.tile([P, b - a, P], F32, name=("bank2", "bank4", "bank3", "bank5", "bank6", "bank0", "bank7")[g])
-            for m in range(a, b):
-                layer2(o_bank[:, m - a, :], m, u)
-            staged = keep.tile([P, b - a, P], F32, name=f"staged{g}")
-            copy = nc.vector.tensor_copy if g in (3, 5) else nc.scalar.copy
-            copy(staged[:], o_bank[:])
-            queue = nc.scalar if g == 6 else nc.sync
-            queue.dma_start(out_view[:, a:b, P * u : P * u + P], staged[:])
+        staged = [keep.tile([P, V], F32, name=f"staged{m}") for m in range(4)]
+        pieces = ((0, 0), (1, 0), (2, 0), (0, 1), (1, 1), (2, 1), (3, 0), (3, 1))
+        for g, (m, u) in enumerate(pieces):
+            cols = slice(P * u, P * u + P)
+            o_bank = psum.tile([P, P], F32, name=("bank2", "bank4", "bank3", "bank5", "bank6", "bank0", "bank7", "bank1")[g])
+            layer2(o_bank[:], m, u)
+            copy = nc.vector.tensor_copy if g in (2, 4, 6) else nc.scalar.copy
+            copy(staged[m][:, cols], o_bank[:])
+            if m < 2:
+                nc.sync.dma_start(out_view[:, m, cols], staged[m][:, cols])
+            elif u == 1:
+                (nc.sync, nc.scalar)[m - 2].dma_start(out_view[:, m, :], staged[m][:])

@@ -30,7 +30,8 @@ def tile_picked_sage_silu_e_kernel(tc, xT, w1, w2, gate, offs, pos1, pos2, pos3,
 
         offs_t = keep.tile([P, S // 16], U16, name="offs_t")
         pos_t = [keep.tile([P, V // 16], U16, name=f"pos_t{d}") for d in range(D)]
-        planes = [keep.tile([P, T], F32, name=f"plane{j}") for j in range(PACK)]
+        first_planes = keep.tile([P, 2, T], F32, name="first_planes")
+        planes = [first_planes[:, 0], first_planes[:, 1]] + [keep.tile([P, T], F32, name=f"plane{j}")[:] for j in (2, 3)]
         w1_raw = [keep.tile([P, PACK, HALF], F32, name=f"w1_raw{b}") for b in range(2)]
         w2_raw = [keep.tile([P, PACK, HALF], F32, name=f"w2_raw{b}") for b in range(2)]
         gate_rows = keep.tile([P, V], F32, name="gate_rows")
@@ -39,11 +40,11 @@ def tile_picked_sage_silu_e_kernel(tc, xT, w1, w2, gate, offs, pos1, pos2, pos3,
         w2_view = w2.rearrange("(p j) m -> p j m", j=PACK)
 
         nc.gpsimd.memset(gate_rows[:], 0.0)
-        for j in range(PACK):
-            nc.sync.dma_start(planes[j][:], x_view[:, j, :])
-            if j == 0:
-                nc.sync.dma_start(gate_rows[0:D, :], gate[:, 0, :])
-                nc.sync.dma_start(offs_t[:], offs)
+        nc.sync.dma_start(first_planes[:], x_view[:, 0:2, :])
+        nc.sync.dma_start(gate_rows[0:D, :], gate[:, 0, :])
+        nc.sync.dma_start(offs_t[:], offs)
+        for j in (2, 3):
+            nc.sync.dma_start(planes[j], x_view[:, j, :])
         for b in range(2):
             nc.sync.dma_start(w1_raw[b][:], w1_view[:, :, HALF * b : HALF * b + HALF])
         for d, pos in enumerate((pos1, pos2, pos3)):
@@ -55,6 +56,12 @@ def tile_picked_sage_silu_e_kernel(tc, xT, w1, w2, gate, offs, pos1, pos2, pos3,
         warm_out = keep.tile([P, 1], F32, name="warm_out")
         nc.vector.memset(warm[:], 0.0)
         nc.scalar.activation(warm_out[:], warm[:], SILU)
+
+        xg = keep.tile([P, S, PACK], BF16, align_bytes=64, name="xg")
+        shared = keep.tile([P, 2, P], F32, name="shared")
+        for j in range(2):
+            nc.scalar.activation(shared[:, j, :], planes[j].indirect(offs_t[:, 24:32]), COPY)
+        nc.scalar.copy(xg[:, S - P :, 0:2], shared[:].rearrange("p j s -> p s j"))
 
         ident = keep.tile([P, P], F32, name="ident")
         make_identity(nc, ident[:])
@@ -70,7 +77,6 @@ def tile_picked_sage_silu_e_kernel(tc, xT, w1, w2, gate, offs, pos1, pos2, pos3,
                 nc.tensor.transpose(spread[:, u, :], gate_cols[:, u, d : d + 1].to_broadcast([P, P]), ident[:])
             nc.scalar.copy(gates[:, d, :], spread[:].rearrange("p u v -> p (u v)"))
 
-        xg = keep.tile([P, S, PACK], BF16, align_bytes=64, name="xg")
         x_codes = keep.tile([P, S], U32, align_bytes=64, name="x_codes")
         x_scales = keep.tile([P, S], U8, align_bytes=64, name="x_scales")
         w1g_low = [keep.tile([P, 64, 2, PACK], BF16, align_bytes=64, name=f"w1g_low{b}") for b in range(2)]
@@ -92,10 +98,11 @@ def tile_picked_sage_silu_e_kernel(tc, xT, w1, w2, gate, offs, pos1, pos2, pos3,
                 stop=True,
             )
 
-        for j in range(PACK - 1):
-            nc.vector.tensor_copy(xg[:, :, j], planes[j][:].indirect(offs_t[:]))
+        for j in range(2):
+            nc.vector.tensor_copy(xg[:, : S - P, j], planes[j].indirect(offs_t[:, 0:24]))
+        nc.vector.tensor_copy(xg[:, :, 2], planes[2].indirect(offs_t[:]))
         for a in range(2):
-            nc.vector.tensor_copy(xg[:, HALF * a : HALF * a + HALF, 3], planes[3][:].indirect(offs_t[:, 16 * a : 16 * a + 16]))
+            nc.vector.tensor_copy(xg[:, HALF * a : HALF * a + HALF, 3], planes[3].indirect(offs_t[:, 16 * a : 16 * a + 16]))
 
         w1_in = [w1_raw[b][:].rearrange("p j (m a t) -> a p m j t", a=2, t=2) for b in range(2)]
 

from contextlib import ExitStack

import concourse.mybir as mybir
from concourse.masks import make_identity

FLOPS = 2 * 512 * 512 * 512 + 2 * 512 * 512 * 256

F32 = mybir.dt.float32
BF16 = mybir.dt.bfloat16
U32 = mybir.dt.uint32
U16 = mybir.dt.uint16
U8 = mybir.dt.uint8
FP8X4 = mybir.dt.float8_e4m3fn_x4
MULT = mybir.AluOpType.mult
ADD = mybir.AluOpType.add
SILU = mybir.ActivationFunctionType.Silu
COPY = mybir.ActivationFunctionType.Copy

P = 128
K, T, S, V, H, N, D = 512, 2048, 512, 256, 512, 512, 3
PACK = 4
HALF = 256


def tile_picked_sage_silu_e_kernel(tc, xT, w1, w2, gate, offs, pos1, pos2, pos3, out):
    nc = tc.nc
    with ExitStack() as ctx:
        keep = ctx.enter_context(tc.tile_pool(name="keep", bufs=1))
        psum = ctx.enter_context(tc.psum_pool(name="psum", bufs=1))

        offs_t = keep.tile([P, S // 16], U16, name="offs_t")
        pos_t = [keep.tile([P, V // 16], U16, name=f"pos_t{d}") for d in range(D)]
        first_planes = keep.tile([P, 2, T], F32, name="first_planes")
        planes = [first_planes[:, 0], first_planes[:, 1]] + [keep.tile([P, T], F32, name=f"plane{j}")[:] for j in (2, 3)]
        w1_raw = [keep.tile([P, PACK, HALF], F32, name=f"w1_raw{b}") for b in range(2)]
        w2_raw = [keep.tile([P, PACK, HALF], F32, name=f"w2_raw{b}") for b in range(2)]
        gate_rows = keep.tile([P, V], F32, name="gate_rows")
        x_view = xT.rearrange("(p j) t -> p j t", j=PACK)
        w1_view = w1.rearrange("(p j) c -> p j c", j=PACK)
        w2_view = w2.rearrange("(p j) m -> p j m", j=PACK)

        nc.gpsimd.memset(gate_rows[:], 0.0)
        nc.sync.dma_start(first_planes[:], x_view[:, 0:2, :])
        nc.sync.dma_start(gate_rows[0:D, :], gate[:, 0, :])
        nc.sync.dma_start(offs_t[:], offs)
        for j in (2, 3):
            nc.sync.dma_start(planes[j], x_view[:, j, :])
        for b in range(2):
            nc.sync.dma_start(w1_raw[b][:], w1_view[:, :, HALF * b : HALF * b + HALF])
        for d, pos in enumerate((pos1, pos2, pos3)):
            nc.sync.dma_start(pos_t[d][:], pos)
        for b in range(2):
            nc.sync.dma_start(w2_raw[b][:], w2_view[:, :, HALF * b : HALF * b + HALF])

        warm = keep.tile([P, 1], F32, name="warm")
        warm_out = keep.tile([P, 1], F32, name="warm_out")
        nc.vector.memset(warm[:], 0.0)
        nc.scalar.activation(warm_out[:], warm[:], SILU)

        xg = keep.tile([P, S, PACK], BF16, align_bytes=64, name="xg")
        shared = keep.tile([P, 2, P], F32, name="shared")
        for j in range(2):
            nc.scalar.activation(shared[:, j, :], planes[j].indirect(offs_t[:, 24:32]), COPY)
        nc.scalar.copy(xg[:, S - P :, 0:2], shared[:].rearrange("p j s -> p s j"))

        ident = keep.tile([P, P], F32, name="ident")
        make_identity(nc, ident[:])
        turned = psum.tile([P, 2, P], F32, name="bank2")
        for u in range(2):
            nc.tensor.transpose(turned[:, u, :], gate_rows[:, P * u : P * u + P], ident[:])
        gate_cols = keep.tile([P, 2, D], F32, name="gate_cols")
        nc.scalar.copy(gate_cols[:], turned[:, :, 0:D])
        gates = keep.tile([P, D, V], F32, name="gates")
        for d in range(D):
            spread = psum.tile([P, 2, P], F32, name=f"bank{d + 2}")
            for u in range(2):
                nc.tensor.transpose(spread[:, u, :], gate_cols[:, u, d : d + 1].to_broadcast([P, P]), ident[:])
            nc.scalar.copy(gates[:, d, :], spread[:].rearrange("p u v -> p (u v)"))

        x_codes = keep.tile([P, S], U32, align_bytes=64, name="x_codes")
        x_scales = keep.tile([P, S], U8, align_bytes=64, name="x_scales")
        w1g_low = [keep.tile([P, 64, 2, PACK], BF16, align_bytes=64, name=f"w1g_low{b}") for b in range(2)]
        w1g_high = keep.tile([P, 2, P, PACK], BF16, align_bytes=64, name="w1g_high")
        w1_codes = [keep.tile([P, w], U32, align_bytes=64, name=f"w1_codes{t}") for t, w in enumerate((P, P, 2 * P))]
        w1_scales = [keep.tile([P, w], U8, align_bytes=64, name=f"w1_scales{t}") for t, w in enumerate((P, P, 2 * P))]

        def quantize(codes, scales, grouped):
            nc.vector.quantize_mx(out=codes.bitcast(FP8X4), scales=scales, in_=grouped)

        def multiply(bank, lhs_codes, lhs_scales, rhs_codes, rhs_scales):
            nc.tensor.matmul_mx(
                out=bank,
                lhsT=lhs_codes.bitcast(FP8X4),
                lhsT_scale=lhs_scales,
                rhs=rhs_codes.bitcast(FP8X4),
                rhs_scale=rhs_scales,
                start=True,
                stop=True,
            )

        for j in range(2):
            nc.vector.tensor_copy(xg[:, : S - P, j], planes[j].indirect(offs_t[:, 0:24]))
        nc.vector.tensor_copy(xg[:, :, 2], planes[2].indirect(offs_t[:]))
        for a in range(2):
            nc.vector.tensor_copy(xg[:, HALF * a : HALF * a + HALF, 3], planes[3].indirect(offs_t[:, 16 * a : 16 * a + 16]))

        w1_in = [w1_raw[b][:].rearrange("p j (m a t) -> a p m j t", a=2, t=2) for b in range(2)]

        def cast_low(b, copy):
            copy(w1g_low[b][:].rearrange("p m t j -> p m j t"), w1_in[b][0])

        def cast_high(b, copy):
            copy(w1g_high[:].rearrange("p t m j -> p m j t")[:, 64 * b : 64 * b + 64], w1_in[b][1])

        def quantize_x(a):
            cols = slice(HALF * a, HALF * a + HALF)
            quantize(x_codes[:, cols], x_scales[:, cols], xg[:, cols, :].rearrange("p s j -> p (s j)"))

        def quantize_low(b):
            quantize(w1_codes[b][:], w1_scales[b][:], w1g_low[b][:].rearrange("p m t j -> p (m t j)"))

        cast_low(0, nc.scalar.copy)
        cast_high(0, nc.scalar.copy)
        quantize_x(0)
        quantize_low(0)
        quantize_x(1)
        cast_low(1, nc.vector.tensor_copy)
        cast_high(1, nc.vector.tensor_copy)
        quantize_low(1)
        quantize(w1_codes[2][:], w1_scales[2][:], w1g_high[:].rearrange("p t m j -> p (t m j)"))

        h = [keep.tile([P, S], F32, align_bytes=64, name=f"h{t}") for t in range(PACK)]

        def layer1(tag, t, cols):
            w = min(t, 2)
            chans = slice(P * (t - w), P * (t - w) + P)
            bank = psum.tile([P, cols.stop - cols.start], F32, name=tag)
            multiply(bank[:], w1_codes[w][:, chans], w1_scales[w][:, chans], x_codes[:, cols], x_scales[:, cols])
            nc.scalar.activation(h[t][:, cols], bank[:], SILU)

        for a in range(2):
            layer1(f"bank{a}", 0, slice(HALF * a, HALF * a + HALF))
        for t in range(1, PACK):
            layer1(f"bank{t + 1}", t, slice(0, S))

        def flip(bank, source, start=True, stop=True):
            nc.tensor.matmul(bank, source, ident[:], is_transpose=True, start=start, stop=stop)

        def fetch_gated(dest, t, d):
            nc.vector.tensor_tensor(dest, h[t][:].indirect(pos_t[d][:]), gates[:, d, :], MULT)

        low_sums = psum.tile([P, 2, 2, P], F32, name="bank3")
        plain_flipped = [psum.tile([P, 2, 2, P], F32, name=f"bank{5 + d}") for d in range(2)]

        def low_term(b, d):
            term = keep.tile([P, V], F32, name=f"term{b}{d}")
            fetch_gated(term[:], b, d)
            for u in range(2):
                flip(low_sums[:, u, b, :], term[:, P * u : P * u + P], (b, d, u) == (0, 0, 0), (b, d, u) == (1, 2, 1))

        def high_term(t, d):
            term = keep.tile([P, V], F32, name=f"plain{t}{d}")
            nc.scalar.activation(term[:], h[2 + t][:].indirect(pos_t[d][:]), COPY)
            for u in range(2):
                flip(plain_flipped[d][:, u, t, :], term[:, P * u : P * u + P])

        for d in range(D):
            low_term(0, d)
        high_term(0, 0)
        low_term(1, 0)
        high_term(1, 0)
        low_term(1, 1)
        high_term(0, 1)
        low_term(1, 2)
        high_term(1, 1)

        parts = [psum.tile([P, 2, P], F32, name=f"bank{u}") for u in range(2)]

        def weigh(d, u):
            weighed = keep.tile([P, 2, P], F32, align_bytes=64, name=f"weighed{d}{u}")
            nc.scalar.activation(weighed[:], plain_flipped[d][:, u], COPY, scale=gate_cols[:, u, d : d + 1])
            for t in range(2):
                flip(parts[u][:, t, :], weighed[:, t, :], (d, t) == (0, 0), (d, t) == (1, 1))

        for u in range(2):
            weigh(0, u)
        low_pairs = keep.tile([P, 2, P], F32, name="low_pairs")
        nc.scalar.copy(low_pairs[:].rearrange("p u w -> p (u w)").bitcast(BF16), low_sums[:].rearrange("p u b c -> p (u b c)"))
        pairs = psum.tile([P, 2, P], F32, name="bank7")
        for u in range(2):
            flip(pairs[:, u, :], low_pairs[:, u, :])
        for u in range(2):
            weigh(1, u)
        zg = [keep.tile([P, P, PACK], BF16, align_bytes=64, name=f"zg{u}") for u in range(2)]
        for u in range(2):
            words = zg[u][:].rearrange("p v j -> p (v j)").bitcast(F32).rearrange("p (v w) -> p v w", w=2)
            nc.scalar.copy(words[:, :, 0], pairs[:, u, :])

        third = keep.tile([P, 2, V], F32, name="third")
        w2g = {}

        def cast_w2(a, b, tag, copy):
            grouped = keep.tile([P, b - a, PACK], BF16, align_bytes=64, name=tag)
            source = w2_raw[a // HALF][:, :, a % HALF : a % HALF + b - a]
            copy(grouped[:].rearrange("p (c i) j -> p c j i", i=2), source.rearrange("p j (c i) -> p c j i", i=2))
            w2g[a] = grouped

        cast_w2(384, 512, "weighed11", nc.scalar.copy)
        fetch_gated(third[:, 0, :], 2, 2)
        cast_w2(0, 256, "h2", nc.vector.tensor_copy)
        fetch_gated(third[:, 1, :], 3, 2)
        cast_w2(256, 384, "h3", nc.vector.tensor_copy)
        w2_codes = keep.tile([P, N], U32, align_bytes=64, name="w2_codes")
        w2_scales = keep.tile([P, N], U8, align_bytes=64, name="w2_scales")

        def quantize_w2(a, b):
            quantize(w2_codes[:, a:b], w2_scales[:, a:b], w2g[a][:].rearrange("p m j -> p (m j)"))

        z_codes = [keep.tile([P, P], U32, align_bytes=64, name=f"z_codes{u}") for u in range(2)]
        z_scales = [keep.tile([P, P], U8, align_bytes=64, name=f"z_scales{u}") for u in range(2)]

        def add_third(u):
            z_out = zg[u][:, :, 2:4].rearrange("p (c i) t -> p c t i", i=2)
            z_in = parts[u][:].rearrange("p t (c i) -> p c t i", i=2)
            last_in = third[:, :, P * u : P * u + P].rearrange("p t (c i) -> p c t i", i=2)
            nc.vector.tensor_tensor(z_out, z_in, last_in, ADD)

        def quantize_z(u):
            quantize(z_codes[u][:], z_scales[u][:], zg[u][:].rearrange("p v j -> p (v j)"))

        add_third(0)
        quantize_w2(0, 256)
        quantize_z(0)
        add_third(1)
        quantize_w2(256, 384)
        quantize_z(1)
        quantize_w2(384, 512)

        def layer2(bank, m, u):
            cols = slice(P * m, P * m + P)
            multiply(bank, w2_codes[:, cols], w2_scales[:, cols], z_codes[u][:], z_scales[u][:])

        out_view = out.rearrange("(m p) v -> p m v", p=P)
        staged = [keep.tile([P, V], F32, name=f"staged{m}") for m in range(4)]
        pieces = ((0, 0), (1, 0), (2, 0), (0, 1), (1, 1), (2, 1), (3, 0), (3, 1))
        for g, (m, u) in enumerate(pieces):
            cols = slice(P * u, P * u + P)
            o_bank = psum.tile([P, P], F32, name=("bank2", "bank4", "bank3", "bank5", "bank6", "bank0", "bank7", "bank1")[g])
            layer2(o_bank[:], m, u)
            copy = nc.vector.tensor_copy if g in (2, 4, 6) else nc.scalar.copy
            copy(staged[m][:, cols], o_bank[:])
            if m < 2:
                nc.sync.dma_start(out_view[:, m, cols], staged[m][:, cols])
            elif u == 1:
                (nc.sync, nc.scalar)[m - 2].dma_start(out_view[:, m, :], staged[m][:])
